import numpy as np
import ml_dtypes


def mxq(x, axis, fmt="e4m3"):
    dtype, down = {"e4m3": (ml_dtypes.float8_e4m3fn, 7), "e5m2": (ml_dtypes.float8_e5m2, 14)}[fmt]
    v = np.moveaxis(np.asarray(x, np.float32).astype(ml_dtypes.bfloat16).astype(np.float64), axis, -1)
    blocks = v.reshape(v.shape[:-1] + (-1, 32))
    amax = np.abs(blocks).max(-1, keepdims=True)
    byte = np.maximum(np.where(amax > 0, np.frexp(amax)[1] - 1 + 127, 0) - down, 1)
    scale = np.exp2(byte - 127.0)
    codes = (blocks / scale).astype(np.float32).astype(dtype).astype(np.float64)
    return np.moveaxis((codes * scale).reshape(v.shape), -1, axis)


WIDE = False


def mx_kscale(k):
    if not WIDE:
        return np.ones(k)
    levels = np.array([10, -10, 5, -5, 0])
    if k % 512:
        return np.exp2(np.random.permutation(np.resize(levels, k // 32))).repeat(32)
    a = np.empty((k // 512, 16))
    for p in range(k // 512):
        a[p, :8] = np.random.permutation(np.resize(levels, 8))
        for g in range(8):
            far = levels[np.abs(levels - a[p, g]) >= 10]
            a[p, g + 8] = far[np.random.randint(len(far))]
    return np.exp2(a.ravel()).repeat(32)


def f64(x):
    return np.asarray(x).astype(np.float64)


def striped(idx):
    return np.tile(idx.reshape(-1, 16).T, (8, 1)).astype(np.uint16)


def unstriped(offs):
    return offs[:16].T.reshape(-1).astype(np.int64)


E2M1 = np.array([0.0, 0.5, 1.0, 1.5, 2.0, 3.0, 4.0, 6.0, -0.0, -0.5, -1.0, -1.5, -2.0, -3.0, -4.0, -6.0])


def pack_weight(w, fmt):
    k, n = w.shape
    w = f64(np.asarray(w, np.float32).astype(ml_dtypes.bfloat16)).reshape(k // 32, 32, n)
    amax = np.abs(w).max(1)
    if fmt == "e4m3":
        byte = np.frexp(amax)[1] - 1 + 127 - 7
    else:
        mant, ex = np.frexp(amax / 6.0)
        byte = np.where(mant > 0.5, ex, ex - 1) + 127
    byte = np.clip(np.where(amax > 0, byte, 1), 1, 254)
    scaled = (w * np.exp2(127.0 - byte)[:, None, :]).reshape(k, n).astype(np.float32)
    by_word = np.ascontiguousarray(scaled.reshape(k // 512, 128, 4, n).transpose(0, 1, 3, 2))
    if fmt == "e4m3":
        words = by_word.astype(ml_dtypes.float8_e4m3fn).view(np.uint8)
    else:
        c = by_word.astype(ml_dtypes.float4_e2m1fn).view(np.uint8) & 0xF
        words = (c[..., 0::2] | (c[..., 1::2] << 4)).reshape(k // 512, 128, 2 * n)
    return np.ascontiguousarray(words), np.ascontiguousarray(byte.astype(np.uint8).reshape(k // 512, 16, n))


def unpack_weight(words, scales, fmt):
    g, _, n = scales.shape
    words = np.ascontiguousarray(words).reshape(g, 128, n, -1)
    if fmt == "e4m3":
        vals = words.view(ml_dtypes.float8_e4m3fn).astype(np.float64)
    else:
        nib = np.empty((g, 128, n, 4), np.uint8)
        nib[..., 0::2] = words & 0xF
        nib[..., 1::2] = words >> 4
        vals = E2M1[nib]
    vals = vals * np.repeat(np.exp2(scales.astype(np.float64) - 127.0), 8, axis=1)[..., None]
    return vals.transpose(0, 1, 3, 2).reshape(g * 512, n)


def gelu(v):
    return 0.5 * v * (1.0 + np.tanh(np.sqrt(2.0 / np.pi) * (v + 0.044715 * v**3)))


K, H, N, T, S, T2, P = 1536, 1024, 768, 2048, 512, 1024, 512


def setup_inputs():
    n = np.random.standard_normal
    s = mx_kscale(K)[:, None]
    u = mx_kscale(H)[:, None]
    tab_words, tab_scales = pack_weight(n((K, T)) * s, "e4m3")
    w2_words, w2_scales = pack_weight(n((H, N)) / np.sqrt(H) / u, "e2m1")
    return {
        "tab_words": tab_words, "tab_scales": tab_scales,
        "offs": striped(np.random.permutation(T)[:S]),
        "offs2": striped(np.random.permutation(T2)[:S]),
        "offs3": striped(np.random.permutation(T2)[:P]),
        "offs4": striped(np.random.permutation(T2)[:P]),
        "w1": (1.6 * n((K, H)) / np.sqrt(K) / s * u.T).astype(np.float32),
        "d": (1.5 * n(H) * u[:, 0]).astype(np.float32),
        "wgs": np.exp(0.3 * n((128, S))).astype(np.float32),
        "page0": (n((H, T2)) * u).astype(np.float32),
        "gm": n((H, P)).astype(np.float32),
        "w2_words": w2_words, "w2_scales": w2_scales,
        "w3": (0.8 * n((H, N)) / np.sqrt(H) / u).astype(np.float32),
    }


def reference(tab_words, tab_scales, offs, offs2, offs3, offs4, w1, d, wgs, page0, gm, w2_words, w2_scales, w3):
    v = unpack_weight(tab_words, tab_scales, "e4m3")[:, unstriped(offs)]
    f = mxq(f64(w1), 0, "e4m3").T @ v
    h = np.maximum(f, f64(d)[:, None] * np.tanh(f))
    before = f64(page0)
    page = before.copy()
    page[:, unstriped(offs2)] = np.tile(f64(wgs), (H // 128, 1)) * h
    x = page[:, unstriped(offs3)] + f64(gm) * before[:, unstriped(offs4)]
    xq = mxq(x, 0, "e4m3")
    e = unpack_weight(w2_words, w2_scales, "e2m1").T @ xq
    y = mxq(f64(w3), 0, "e4m3").T @ xq
    return e / (1.0 + np.exp(-e)) + y

@@ -1,0 +1,336 @@
+from contextlib import ExitStack
+
+import concourse.mybir as mybir
+
+K, H, N, T, S, T2, M = 1536, 1024, 768, 2048, 512, 1024, 512
+FLOPS = 2 * K * H * S + 2 * 2 * H * N * M
+
+F32 = mybir.dt.float32
+BF16 = mybir.dt.bfloat16
+I32 = mybir.dt.int32
+U32 = mybir.dt.uint32
+U16 = mybir.dt.uint16
+U8 = mybir.dt.uint8
+FP8X4 = mybir.dt.float8_e4m3fn_x4
+FP4X4 = mybir.dt.float4_e2m1fn_x4
+ACT = mybir.ActivationFunctionType
+ALU = mybir.AluOpType
+
+P = 128
+PACK = 4
+PASS = P * PACK
+QUAD = 32
+K_PASSES = K // PASS
+H_PASSES = H // PASS
+SLICES = H_PASSES * PACK
+N_TILES = N // P
+N_HALF = N // 2
+M_HALF = M // 2
+
+
+def tile_list_penstock_blister_scores_kernel(
+    tc, tab_words, tab_scales, offs, offs2, offs3, offs4, w1, d, wgs, page0, gm, w2_words, w2_scales, w3, out
+):
+    nc = tc.nc
+    with ExitStack() as ctx:
+        keep = ctx.enter_context(tc.tile_pool(name="keep", bufs=1))
+        raw_pool = ctx.enter_context(tc.tile_pool(name="raw", bufs=4))
+        grouped_pool = ctx.enter_context(tc.tile_pool(name="grouped", bufs=3))
+        pair_pool = ctx.enter_context(tc.tile_pool(name="pair", bufs=2))
+        h_pool = ctx.enter_context(tc.tile_pool(name="h", bufs=6))
+        old_pool = ctx.enter_context(tc.tile_pool(name="old", bufs=6))
+        silu_pool = ctx.enter_context(tc.tile_pool(name="silu", bufs=4))
+        psum = ctx.enter_context(tc.psum_pool(name="psum", bufs=8))
+
+        def held(name, shape, dtype):
+            return keep.tile(shape, dtype, name=name, align_bytes=64)
+
+        idx = held("idx", [P, S // 16], U16)
+        idx2 = held("idx2", [P, S // 16], U16)
+        idx3 = held("idx3", [P, M // 16], U16)
+        idx4 = held("idx4", [P, M // 16], U16)
+        tab_w = [held("tab_w%d" % a, [P, T], U32) for a in range(K_PASSES)]
+        tab_s = held("tab_s", [P, T], U8)
+        v_w = [held("v_w%d" % a, [P, S], U32) for a in range(K_PASSES)]
+        v_s = held("v_s", [P, S], U8)
+        w1_w = {}
+        w1_s = {}
+        page = [held("page%d" % s, [P, T2], F32) for s in range(SLICES)]
+        gm_sb = [held("gm%d" % i, [P, 2, M], F32) for i in range(SLICES // 2)]
+        wgs_sb = [held("wgs%d" % i, [P, 2, S], F32) for i in range(2)]
+        x32 = {}
+        d_sb = held("d_sb", [P, H_PASSES, PACK], F32)
+        w2_w = held("w2_w", [P, H_PASSES, 2 * N], U8)
+        w2_s = held("w2_s", [P, H_PASSES, N], U8)
+        w3_w = {}
+        w3_s = {}
+        x16 = [held("x16_%d" % b, [P, M, PACK], BF16) for b in range(H_PASSES)]
+        x_w = [held("x_w%d" % b, [P, M], U32) for b in range(H_PASSES)]
+        x_s = [held("x_s%d" % b, [P, M], U8) for b in range(H_PASSES)]
+        raw = {}
+        grouped = {}
+        f_bank = {}
+        tanh_f = {}
+        h = {}
+        old = {}
+
+        nc.vector.memset(tab_s[:].bitcast(I32), 0)
+        for q in range(P // QUAD):
+            nc.scalar.dma_start(
+                out=tab_s[QUAD * q : QUAD * q + 4 * K_PASSES, :].bitcast(I32),
+                in_=tab_scales[:, 4 * q : 4 * q + 4, :].bitcast(I32),
+            )
+        nc.gpsimd.dma_start(out=d_sb[:], in_=d.rearrange("(b p t) -> p b t", b=H_PASSES, t=PACK))
+        nc.gpsimd.memset(w2_s[:].rearrange("p a c -> p (a c)").bitcast(I32), 0)
+        for q in range(P // QUAD):
+            nc.gpsimd.dma_start(
+                out=w2_s[QUAD * q : QUAD * q + 4, :, :].bitcast(I32),
+                in_=w2_scales[:, 4 * q : 4 * q + 4, :].rearrange("a q c -> q a c").bitcast(I32),
+            )
+
+        def load_w1(a, b):
+            raw["w1", a, b] = raw_pool.tile([P, PACK, PASS], F32, name="raw")
+            rows = w1[a * PASS : (a + 1) * PASS, b * PASS : (b + 1) * PASS]
+            nc.sync.dma_start(out=raw["w1", a, b][:], in_=rows.rearrange("(p j) c -> p j c", j=PACK))
+
+        def load_w3(b, half):
+            raw["w3", b, half] = raw_pool.tile([P, PACK, N_HALF], F32, name="raw")
+            rows = w3[b * PASS : (b + 1) * PASS, half * N_HALF : (half + 1) * N_HALF]
+            nc.sync.dma_start(out=raw["w3", b, half][:], in_=rows.rearrange("(p j) c -> p j c", j=PACK))
+
+        def load_tab(a):
+            nc.sync.dma_start(
+                out=tab_w[a][:].bitcast(I32), in_=tab_words[a].rearrange("p t i -> p (t i)").bitcast(I32)
+            )
+
+        def load_page(s):
+            b, t = divmod(s, PACK)
+            rows = page0[b * PASS : (b + 1) * PASS, :].rearrange("(p t) c -> p t c", t=PACK)
+            nc.sync.dma_start(out=page[s][:], in_=rows[:, t, :])
+
+        def load_gm(i):
+            b, t = divmod(2 * i, PACK)
+            rows = gm[b * PASS : (b + 1) * PASS, :].rearrange("(p t) m -> p t m", t=PACK)
+            nc.sync.dma_start(out=gm_sb[i][:], in_=rows[:, t : t + 2, :])
+
+        def load_wgs(i):
+            rows = wgs.rearrange("(q t) j -> q t j", t=PACK)
+            for q in range(P // QUAD):
+                nc.sync.dma_start(out=wgs_sb[i][QUAD * q : QUAD * (q + 1), :, :], in_=rows[:, 2 * i : 2 * i + 2, :])
+
+        def round_w1(a, b):
+            grouped["w1", a, b] = grouped_pool.tile([P, PASS * PACK], BF16, name="grouped", align_bytes=64)
+            nc.scalar.copy(
+                out=grouped["w1", a, b][:].rearrange("p (t m j) -> p m j t", t=PACK, j=PACK),
+                in_=raw["w1", a, b][:].rearrange("p j (m t) -> p m j t", t=PACK),
+            )
+
+        def quantise_w1(a, b):
+            w1_w[a, b] = held("w1_w%d%d" % (a, b), [P, PASS], U32)
+            w1_s[a, b] = held("w1_s%d%d" % (a, b), [P, PASS], U8)
+            nc.vector.quantize_mx(out=w1_w[a, b][:].bitcast(FP8X4), scales=w1_s[a, b][:], in_=grouped["w1", a, b][:])
+
+        def round_w3(b, half):
+            grouped["w3", b, half] = grouped_pool.tile([P, N_HALF * PACK], BF16, name="grouped", align_bytes=64)
+            nc.scalar.copy(
+                out=grouped["w3", b, half][:].rearrange("p (c i j) -> p c j i", i=4, j=PACK),
+                in_=raw["w3", b, half][:].rearrange("p j (c i) -> p c j i", i=4),
+            )
+
+        def quantise_w3(b, half):
+            w3_w[b, half] = held("w3_w%d%d" % (b, half), [P, N_HALF], U32)
+            w3_s[b, half] = held("w3_s%d%d" % (b, half), [P, N_HALF], U8)
+            nc.vector.quantize_mx(
+                out=w3_w[b, half][:].bitcast(FP8X4), scales=w3_s[b, half][:], in_=grouped["w3", b, half][:]
+            )
+
+        def gather_words(a):
+            nc.vector.tensor_copy(out=v_w[a][:], in_=tab_w[a][:].indirect(idx[:]))
+
+        def first_product(s):
+            b, t = divmod(s, PACK)
+            f_bank[s] = psum.tile([P, S], F32, name="bank")
+            cols = slice(t * P, (t + 1) * P)
+            for a in range(K_PASSES):
+                nc.tensor.matmul_mx(
+                    out=f_bank[s][:],
+                    lhsT=w1_w[a, b][:, cols].bitcast(FP8X4),
+                    lhsT_scale=w1_s[a, b][:, cols],
+                    rhs=v_w[a][:].bitcast(FP8X4),
+                    rhs_scale=v_s[4 * a : P, :],
+                    start=(a == 0),
+                    stop=(a == K_PASSES - 1),
+                )
+
+        def tanh_of(s):
+            tanh_f[s] = pair_pool.tile([P, S], F32, name="tanh_f")
+            nc.scalar.activation(out=tanh_f[s][:], in_=f_bank[s][:], func=ACT.Tanh)
+
+        def feature(s):
+            b, t = divmod(s, PACK)
+            h[s] = h_pool.tile([P, S], F32, name="h")
+            nc.vector.scalar_tensor_tensor(
+                out=h[s][:], in0=tanh_f[s][:], scalar=d_sb[:, b, t : t + 1], in1=f_bank[s][:], op0=ALU.mult, op1=ALU.max
+            )
+
+        def fetch_old(s):
+            old[s] = old_pool.tile([P, M], F32, name="old")
+            nc.vector.tensor_tensor(
+                out=old[s][:], in0=page[s][:].indirect(idx4[:]), in1=gm_sb[s // 2][:, s % 2, :], op=ALU.mult
+            )
+
+        def put(s):
+            t = s % PACK
+            nc.vector.tensor_tensor(
+                out=page[s][:].indirect(idx2[:]), in0=h[s][:], in1=wgs_sb[t // 2][:, t % 2, :], op=ALU.mult
+            )
+
+        def fetch_new(s, m0, m1):
+            b, t = divmod(s, PACK)
+            nc.vector.tensor_tensor(
+                out=x32[b, m0][:, t, :],
+                in0=page[s][:].indirect(idx3[:, m0 // 16 : m1 // 16]),
+                in1=old[s][:, m0:m1],
+                op=ALU.add,
+            )
+
+        def round_x(b, m0, m1):
+            nc.scalar.copy(
+                out=x16[b][:, m0:m1, :].rearrange("p (c i) t -> p c t i", i=4),
+                in_=x32[b, m0][:].rearrange("p t (c i) -> p c t i", i=4),
+            )
+
+        def quantise_x(b, m0, m1):
+            nc.vector.quantize_mx(
+                out=x_w[b][:, m0:m1].bitcast(FP8X4),
+                scales=x_s[b][:, m0:m1],
+                in_=x16[b][:, m0:m1, :].rearrange("p m t -> p (m t)"),
+            )
+
+        score_bank = {}
+
+        def score_pass(n, half, b):
+            if b == 0:
+                score_bank[n, half] = psum.tile([P, 2, M_HALF], F32, name="bank")
+            bank = score_bank[n, half]
+            cols = slice(half * M_HALF, (half + 1) * M_HALF)
+            nc.tensor.matmul_mx(
+                out=bank[:, 0, :],
+                lhsT=w2_w[:, b, 2 * P * n : 2 * P * (n + 1)].bitcast(FP4X4),
+                lhsT_scale=w2_s[:, b, P * n : P * (n + 1)],
+                rhs=x_w[b][:, cols].bitcast(FP8X4),
+                rhs_scale=x_s[b][:, cols],
+                start=(b == 0),
+                stop=False,
+            )
+            w_half, w_tile = divmod(n, N_TILES // 2)
+            nc.tensor.matmul_mx(
+                out=bank[:, 1, :],
+                lhsT=w3_w[b, w_half][:, P * w_tile : P * (w_tile + 1)].bitcast(FP8X4),
+                lhsT_scale=w3_s[b, w_half][:, P * w_tile : P * (w_tile + 1)],
+                rhs=x_w[b][:, cols].bitcast(FP8X4),
+                rhs_scale=x_s[b][:, cols],
+                start=False,
+                stop=(b == H_PASSES - 1),
+            )
+
+        def finish(n, half):
+            bank = score_bank[n, half]
+            gated = silu_pool.tile([P, M_HALF], F32, name="gated")
+            nc.scalar.activation(out=gated[:], in_=bank[:, 0, :], func=ACT.Silu)
+            result = held("result%d%d" % (n, half), [P, M_HALF], F32)
+            nc.vector.tensor_tensor(out=result[:], in0=bank[:, 1, :], in1=gated[:], op=ALU.add)
+            nc.sync.dma_start(out=out[P * n : P * (n + 1), half * M_HALF : (half + 1) * M_HALF], in_=result[:])
+
+        def load_pair(i):
+            load_page(2 * i)
+            load_page(2 * i + 1)
+            load_gm(i)
+
+        def features(b):
+            for s in range(PACK * b, PACK * (b + 1)):
+                first_product(s)
+                tanh_of(s)
+                feature(s)
+
+        def rewrite_pair(i, m1):
+            for s in (2 * i, 2 * i + 1):
+                put(s)
+            for s in (2 * i, 2 * i + 1):
+                fetch_new(s, 0, m1)
+
+        for a in range(K_PASSES):
+            load_w1(a, 0)
+        nc.sync.dma_start(idx[:], offs)
+        for a in range(K_PASSES):
+            load_tab(a)
+        nc.sync.dma_start(idx4[:], offs4)
+        load_pair(0)
+        nc.sync.dma_start(idx2[:], offs2)
+        nc.sync.dma_start(idx3[:], offs3)
+        load_wgs(0)
+
+        for a in range(K_PASSES):
+            round_w1(a, 0)
+            quantise_w1(a, 0)
+        nc.vector.tensor_copy(out=v_s[:], in_=tab_s[:].indirect(idx[:]))
+        for a in range(K_PASSES):
+            gather_words(a)
+        features(0)
+        fetch_old(0)
+        fetch_old(1)
+
+        x32[0, 0] = held("x32_a", [P, PACK, M], F32)
+        x32[1, 0] = held("x32_b", [P, PACK, M_HALF], F32)
+        rewrite_pair(0, M)
+
+        for a in range(K_PASSES):
+            load_w1(a, 1)
+        load_pair(1)
+        load_wgs(1)
+        load_pair(2)
+        for a in range(K_PASSES):
+            round_w1(a, 1)
+            quantise_w1(a, 1)
+        fetch_old(2)
+        fetch_old(3)
+        features(1)
+        rewrite_pair(1, M)
+        round_x(0, 0, M)
+
+        for b in range(H_PASSES):
+            for half in range(2):
+                load_w3(b, half)
+        nc.sync.dma_start(out=w2_w[:].bitcast(I32), in_=w2_words.rearrange("a p c -> p a c").bitcast(I32))
+        load_pair(3)
+
+        fetch_old(4)
+        fetch_old(5)
+        rewrite_pair(2, M_HALF)
+        quantise_x(0, 0, M)
+        for b in range(H_PASSES):
+            for half in range(2):
+                round_w3(b, half)
+                quantise_w3(b, half)
+        for n in range(N_TILES):
+            score_pass(n, 0, 0)
+        fetch_old(6)
+        fetch_old(7)
+        rewrite_pair(3, M_HALF)
+
+        round_x(1, 0, M_HALF)
+        x32[1, M_HALF] = held("wgs1", [P, PACK, M_HALF], F32)
+        for s in range(PACK, SLICES):
+            fetch_new(s, M_HALF, M)
+        quantise_x(1, 0, M_HALF)
+        round_x(1, M_HALF, M)
+        for n in range(N_TILES):
+            score_pass(n, 0, 1)
+        quantise_x(1, M_HALF, M)
+        for n in range(N_TILES):
+            finish(n, 0)
+        for n in range(N_TILES):
+            score_pass(n, 1, 0)
+            score_pass(n, 1, 1)
+        for n in range(N_TILES):
+            finish(n, 1)

@@ -1,6 +1,7 @@
 from contextlib import ExitStack
 
 import concourse.mybir as mybir
+from concourse.masks import make_identity
 
 K, H, N, T, S, T2, M = 1536, 1024, 768, 2048, 512, 1024, 512
 FLOPS = 2 * K * H * S + 2 * 2 * H * N * M
@@ -34,10 +35,10 @@ def tile_list_penstock_blister_scores_kernel(
     nc = tc.nc
     with ExitStack() as ctx:
         keep = ctx.enter_context(tc.tile_pool(name="keep", bufs=1))
-        raw_pool = ctx.enter_context(tc.tile_pool(name="raw", bufs=4))
-        grouped_pool = ctx.enter_context(tc.tile_pool(name="grouped", bufs=3))
-        pair_pool = ctx.enter_context(tc.tile_pool(name="pair", bufs=2))
-        h_pool = ctx.enter_context(tc.tile_pool(name="h", bufs=6))
+        raw_pool = ctx.enter_context(tc.tile_pool(name="raw", bufs=6))
+        grouped_pool = ctx.enter_context(tc.tile_pool(name="grouped", bufs=4))
+        tanh_pool = ctx.enter_context(tc.tile_pool(name="tanh", bufs=4))
+        h_pool = ctx.enter_context(tc.tile_pool(name="h", bufs=3))
         old_pool = ctx.enter_context(tc.tile_pool(name="old", bufs=6))
         silu_pool = ctx.enter_context(tc.tile_pool(name="silu", bufs=4))
         psum = ctx.enter_context(tc.psum_pool(name="psum", bufs=8))
@@ -53,26 +54,32 @@ def tile_list_penstock_blister_scores_kernel(
         tab_s = held("tab_s", [P, T], U8)
         v_w = [held("v_w%d" % a, [P, S], U32) for a in range(K_PASSES)]
         v_s = held("v_s", [P, S], U8)
-        w1_w = {}
-        w1_s = {}
         page = [held("page%d" % s, [P, T2], F32) for s in range(SLICES)]
-        gm_sb = [held("gm%d" % i, [P, 2, M], F32) for i in range(SLICES // 2)]
-        wgs_sb = [held("wgs%d" % i, [P, 2, S], F32) for i in range(2)]
-        x32 = {}
-        d_sb = held("d_sb", [P, H_PASSES, PACK], F32)
+        gm_low = [held("gm_low%d" % s, [P, M], F32) for s in range(PACK)]
+        gm_high = [held("gm_high%d" % i, [P, 2, M], F32) for i in range(2)]
+        wgs_low = held("wgs_low", [P, S], F32)
+        wgs_high = [held("wgs_high%d" % i, [P, 2, S], F32) for i in range(2)]
+        d_sb = [held("d_sb%d" % b, [P, PACK], F32) for b in range(H_PASSES)]
         w2_w = held("w2_w", [P, H_PASSES, 2 * N], U8)
         w2_s = held("w2_s", [P, H_PASSES, N], U8)
+        x16 = {key: held("x16_%d%d" % key, [P, M_HALF * PACK], BF16)[:] for key in ((0, 0), (0, M_HALF), (1, M_HALF))}
+        ident = held("ident", [P, P], F32)
+        x_rows = {}
+        x_s = [held("x_s%d" % b, [P, M], U8) for b in range(H_PASSES)]
+        x_w = {}
+        x_low = {}
+        x32 = {}
+        w1_ops = {}
         w3_w = {}
         w3_s = {}
-        x16 = [held("x16_%d" % b, [P, M, PACK], BF16) for b in range(H_PASSES)]
-        x_w = [held("x_w%d" % b, [P, M], U32) for b in range(H_PASSES)]
-        x_s = [held("x_s%d" % b, [P, M], U8) for b in range(H_PASSES)]
         raw = {}
         grouped = {}
         f_bank = {}
         tanh_f = {}
         h = {}
         old = {}
+        result = {}
+        score_bank = {}
 
         nc.vector.memset(tab_s[:].bitcast(I32), 0)
         for q in range(P // QUAD):
@@ -80,7 +87,12 @@ def tile_list_penstock_blister_scores_kernel(
                 out=tab_s[QUAD * q : QUAD * q + 4 * K_PASSES, :].bitcast(I32),
                 in_=tab_scales[:, 4 * q : 4 * q + 4, :].bitcast(I32),
             )
-        nc.gpsimd.dma_start(out=d_sb[:], in_=d.rearrange("(b p t) -> p b t", b=H_PASSES, t=PACK))
+        warm = held("warm", [P, 2], F32)
+        nc.vector.memset(warm[:, 0:1], 0.0)
+        nc.scalar.activation(out=warm[:, 1:2], in_=warm[:, 0:1], func=ACT.Silu)
+        with nc.allow_non_contiguous_dma(reason="one value of d for each partition and slice"):
+            nc.gpsimd.dma_start(out=d_sb[0][:], in_=d[0:PASS].rearrange("(c p) -> p c", p=P))
+        nc.gpsimd.dma_start(out=d_sb[1][:], in_=d[PASS:H].rearrange("(p t) -> p t", t=PACK))
         nc.gpsimd.memset(w2_s[:].rearrange("p a c -> p (a c)").bitcast(I32), 0)
         for q in range(P // QUAD):
             nc.gpsimd.dma_start(
@@ -88,15 +100,27 @@ def tile_list_penstock_blister_scores_kernel(
                 in_=w2_scales[:, 4 * q : 4 * q + 4, :].rearrange("a q c -> q a c").bitcast(I32),
             )
 
-        def load_w1(a, b):
-            raw["w1", a, b] = raw_pool.tile([P, PACK, PASS], F32, name="raw")
-            rows = w1[a * PASS : (a + 1) * PASS, b * PASS : (b + 1) * PASS]
-            nc.sync.dma_start(out=raw["w1", a, b][:], in_=rows.rearrange("(p j) c -> p j c", j=PACK))
+        make_identity(nc, ident[:])
+
+        def load_w1_low(c0, width, a0, a1):
+            key = ("low", c0, a0)
+            raw[key] = raw_pool.tile([P, a1 - a0, PACK, width], F32, name="raw")
+            for a in range(a0, a1):
+                rows = w1[a * PASS : (a + 1) * PASS, c0 : c0 + width]
+                nc.sync.dma_start(out=raw[key][:, a - a0, :, :], in_=rows.rearrange("(p j) c -> p j c", j=PACK))
+
+        def load_w1_high(a):
+            raw["high", a] = raw_pool.tile([P, PACK, PASS], F32, name="raw")
+            rows = w1[a * PASS : (a + 1) * PASS, PASS:H]
+            nc.sync.dma_start(out=raw["high", a][:], in_=rows.rearrange("(p j) c -> p j c", j=PACK))
 
         def load_w3(b, half):
             raw["w3", b, half] = raw_pool.tile([P, PACK, N_HALF], F32, name="raw")
             rows = w3[b * PASS : (b + 1) * PASS, half * N_HALF : (half + 1) * N_HALF]
             nc.sync.dma_start(out=raw["w3", b, half][:], in_=rows.rearrange("(p j) c -> p j c", j=PACK))
+
+        def load_w2():
+            nc.sync.dma_start(out=w2_w[:].bitcast(I32), in_=w2_words.rearrange("a p c -> p a c").bitcast(I32))
 
         def load_tab(a):
             nc.sync.dma_start(
@@ -104,31 +128,57 @@ def tile_list_penstock_blister_scores_kernel(
             )
 
         def load_page(s):
-            b, t = divmod(s, PACK)
-            rows = page0[b * PASS : (b + 1) * PASS, :].rearrange("(p t) c -> p t c", t=PACK)
-            nc.sync.dma_start(out=page[s][:], in_=rows[:, t, :])
+            if s < PACK:
+                rows = page0[s * P : (s + 1) * P, :]
+            else:
+                rows = page0[PASS:H, :].rearrange("(p t) c -> p t c", t=PACK)[:, s - PACK, :]
+            nc.sync.dma_start(out=page[s][:], in_=rows)
 
-        def load_gm(i):
-            b, t = divmod(2 * i, PACK)
-            rows = gm[b * PASS : (b + 1) * PASS, :].rearrange("(p t) m -> p t m", t=PACK)
-            nc.sync.dma_start(out=gm_sb[i][:], in_=rows[:, t : t + 2, :])
+        def load_gm_low(s):
+            nc.sync.dma_start(out=gm_low[s][:], in_=gm[s * P : (s + 1) * P, :])
 
-        def load_wgs(i):
+        def load_gm_high(i):
+            rows = gm[PASS:H, :].rearrange("(p t) m -> p t m", t=PACK)
+            nc.sync.dma_start(out=gm_high[i][:], in_=rows[:, 2 * i : 2 * i + 2, :])
+
+        def load_wgs_high(i):
             rows = wgs.rearrange("(q t) j -> q t j", t=PACK)
-            for q in range(P // QUAD):
-                nc.sync.dma_start(out=wgs_sb[i][QUAD * q : QUAD * (q + 1), :, :], in_=rows[:, 2 * i : 2 * i + 2, :])
+            for q in (0, 2, 1, 3):
+                nc.sync.dma_start(
+                    out=wgs_high[i][QUAD * q : QUAD * (q + 1), :, :], in_=rows[:, 2 * i : 2 * i + 2, :]
+                )
 
-        def round_w1(a, b):
-            grouped["w1", a, b] = grouped_pool.tile([P, PASS * PACK], BF16, name="grouped", align_bytes=64)
+        def round_w1_low(c0, width, a0, a1):
+            key = ("low", c0, a0)
+            grouped[key] = grouped_pool.tile([P, (a1 - a0) * width * PACK], BF16, name="grouped", align_bytes=64)
             nc.scalar.copy(
-                out=grouped["w1", a, b][:].rearrange("p (t m j) -> p m j t", t=PACK, j=PACK),
-                in_=raw["w1", a, b][:].rearrange("p j (m t) -> p m j t", t=PACK),
+                out=grouped[key][:].rearrange("p (a c i j) -> p a c j i", a=a1 - a0, i=4, j=PACK),
+                in_=raw[key][:].rearrange("p a j (c i) -> p a c j i", i=4),
             )
 
-        def quantise_w1(a, b):
-            w1_w[a, b] = held("w1_w%d%d" % (a, b), [P, PASS], U32)
-            w1_s[a, b] = held("w1_s%d%d" % (a, b), [P, PASS], U8)
-            nc.vector.quantize_mx(out=w1_w[a, b][:].bitcast(FP8X4), scales=w1_s[a, b][:], in_=grouped["w1", a, b][:])
+        def quantise_w1_low(c0, width, a0, a1):
+            key = ("low", c0, a0)
+            words = held("w1_w%d_%d" % (c0, a0), [P, (a1 - a0) * width], U32)
+            scales = held("w1_s%d_%d" % (c0, a0), [P, (a1 - a0) * width], U8)
+            nc.vector.quantize_mx(out=words[:].bitcast(FP8X4), scales=scales[:], in_=grouped[key][:])
+            for a in range(a0, a1):
+                for c in range(width // P):
+                    cols = slice((a - a0) * width + c * P, (a - a0) * width + (c + 1) * P)
+                    w1_ops[c0 // P + c, a] = (words[:, cols], scales[:, cols])
+
+        def round_w1_high(a):
+            grouped["high", a] = grouped_pool.tile([P, PASS * PACK], BF16, name="grouped", align_bytes=64)
+            nc.scalar.copy(
+                out=grouped["high", a][:].rearrange("p (t m j) -> p m j t", t=PACK, j=PACK),
+                in_=raw["high", a][:].rearrange("p j (m t) -> p m j t", t=PACK),
+            )
+
+        def quantise_w1_high(a):
+            words = held("w1_high_w%d" % a, [P, PASS], U32)
+            scales = held("w1_high_s%d" % a, [P, PASS], U8)
+            nc.vector.quantize_mx(out=words[:].bitcast(FP8X4), scales=scales[:], in_=grouped["high", a][:])
+            for t in range(PACK):
+                w1_ops[PACK + t, a] = (words[:, t * P : (t + 1) * P], scales[:, t * P : (t + 1) * P])
 
         def round_w3(b, half):
             grouped["w3", b, half] = grouped_pool.tile([P, N_HALF * PACK], BF16, name="grouped", align_bytes=64)
@@ -138,97 +188,119 @@ def tile_list_penstock_blister_scores_kernel(
             )
 
         def quantise_w3(b, half):
-            w3_w[b, half] = held("w3_w%d%d" % (b, half), [P, N_HALF], U32)
+            if (b, half) not in w3_w:
+                w3_w[b, half] = held("w3_w%d%d" % (b, half), [P, N_HALF], U32)[:]
             w3_s[b, half] = held("w3_s%d%d" % (b, half), [P, N_HALF], U8)
             nc.vector.quantize_mx(
-                out=w3_w[b, half][:].bitcast(FP8X4), scales=w3_s[b, half][:], in_=grouped["w3", b, half][:]
+                out=w3_w[b, half].bitcast(FP8X4), scales=w3_s[b, half][:], in_=grouped["w3", b, half][:]
             )
+
+        def gather_scales():
+            nc.vector.tensor_copy(out=v_s[:], in_=tab_s[:].indirect(idx[:]))
 
         def gather_words(a):
             nc.vector.tensor_copy(out=v_w[a][:], in_=tab_w[a][:].indirect(idx[:]))
 
-        def first_product(s):
-            b, t = divmod(s, PACK)
+        def feature(s):
             f_bank[s] = psum.tile([P, S], F32, name="bank")
-            cols = slice(t * P, (t + 1) * P)
             for a in range(K_PASSES):
+                words, scales = w1_ops[s, a]
                 nc.tensor.matmul_mx(
                     out=f_bank[s][:],
-                    lhsT=w1_w[a, b][:, cols].bitcast(FP8X4),
-                    lhsT_scale=w1_s[a, b][:, cols],
+                    lhsT=words.bitcast(FP8X4),
+                    lhsT_scale=scales,
                     rhs=v_w[a][:].bitcast(FP8X4),
                     rhs_scale=v_s[4 * a : P, :],
                     start=(a == 0),
                     stop=(a == K_PASSES - 1),
                 )
-
-        def tanh_of(s):
-            tanh_f[s] = pair_pool.tile([P, S], F32, name="tanh_f")
+            tanh_f[s] = tanh_pool.tile([P, S], F32, name="tanh_f")
             nc.scalar.activation(out=tanh_f[s][:], in_=f_bank[s][:], func=ACT.Tanh)
-
-        def feature(s):
-            b, t = divmod(s, PACK)
-            h[s] = h_pool.tile([P, S], F32, name="h")
+            if s == SLICES - 1:
+                h[s] = held("h_last", [P, S], F32)
+            elif s == PACK:
+                h[s] = held("h_mid", [P, S], F32)
+            elif s == 0:
+                h[s] = held("gm_low0", [P, S], F32)
+            else:
+                h[s] = h_pool.tile([P, S], F32, name="h")
             nc.vector.scalar_tensor_tensor(
-                out=h[s][:], in0=tanh_f[s][:], scalar=d_sb[:, b, t : t + 1], in1=f_bank[s][:], op0=ALU.mult, op1=ALU.max
+                out=h[s][:], in0=tanh_f[s][:], scalar=d_sb[s // PACK][:, s % PACK : s % PACK + 1], in1=f_bank[s][:], op0=ALU.mult, op1=ALU.max
             )
 
         def fetch_old(s):
             old[s] = old_pool.tile([P, M], F32, name="old")
-            nc.vector.tensor_tensor(
-                out=old[s][:], in0=page[s][:].indirect(idx4[:]), in1=gm_sb[s // 2][:, s % 2, :], op=ALU.mult
-            )
+            factor = gm_low[s][:] if s < PACK else gm_high[(s - PACK) // 2][:, s % 2, :]
+            nc.vector.tensor_tensor(out=old[s][:], in0=page[s][:].indirect(idx4[:]), in1=factor, op=ALU.mult)
 
         def put(s):
-            t = s % PACK
-            nc.vector.tensor_tensor(
-                out=page[s][:].indirect(idx2[:]), in0=h[s][:], in1=wgs_sb[t // 2][:, t % 2, :], op=ALU.mult
+            factor = wgs_low[:] if s < PACK else wgs_high[(s - PACK) // 2][:, s % 2, :]
+            nc.vector.tensor_tensor(out=page[s][:].indirect(idx2[:]), in0=h[s][:], in1=factor, op=ALU.mult)
+
+        def fetch_new_low(s):
+            x_low[s] = held("gm_low%d" % ((s + 1) % PACK), [P, M], F32)
+            nc.vector.tensor_tensor(out=x_low[s][:], in0=page[s][:].indirect(idx3[:]), in1=old[s][:], op=ALU.add)
+
+        def turn_x_low(s):
+            bank = psum.tile([P, PACK, P], F32, name="bank")
+            for c in range(M // P):
+                nc.tensor.transpose(bank[:, c, :], x_low[s][:, c * P : (c + 1) * P], ident[:])
+            nc.scalar.copy(out=x_rows[0][:, :, s * P : (s + 1) * P], in_=bank[:])
+
+        def turn_x_back(i):
+            bank = psum.tile([P, 2, 2, P], F32, name="bank")
+            for c in range(2):
+                words = x_rows[0][:, 2 * i + c, :].bitcast(F32)
+                for u in range(2):
+                    nc.tensor.transpose(bank[:, c, u, :], words[:, u : PASS // 2 : 2], ident[:])
+            half = x16[0, i * M_HALF].bitcast(F32)
+            nc.scalar.copy(
+                out=half.rearrange("p (c m u) -> p c m u", c=2, u=2), in_=bank[:].rearrange("p c u m -> p c m u")
             )
 
         def fetch_new(s, m0, m1):
-            b, t = divmod(s, PACK)
             nc.vector.tensor_tensor(
-                out=x32[b, m0][:, t, :],
+                out=x32[1, m0][:, s - PACK, :],
                 in0=page[s][:].indirect(idx3[:, m0 // 16 : m1 // 16]),
                 in1=old[s][:, m0:m1],
                 op=ALU.add,
             )
 
-        def round_x(b, m0, m1):
-            nc.scalar.copy(
-                out=x16[b][:, m0:m1, :].rearrange("p (c i) t -> p c t i", i=4),
-                in_=x32[b, m0][:].rearrange("p t (c i) -> p c t i", i=4),
-            )
+        def round_x(b, m0, m1, on_vector):
+            dst = x16[b, m0].rearrange("p (c i t) -> p c t i", i=4, t=PACK)
+            src = x32[b, m0].rearrange("p t (c i) -> p c t i", i=4)
+            if on_vector:
+                nc.vector.tensor_copy(out=dst, in_=src)
+            else:
+                nc.scalar.copy(out=dst, in_=src)
 
         def quantise_x(b, m0, m1):
             nc.vector.quantize_mx(
-                out=x_w[b][:, m0:m1].bitcast(FP8X4),
+                out=x_w[b, m0 // M_HALF].bitcast(FP8X4),
                 scales=x_s[b][:, m0:m1],
-                in_=x16[b][:, m0:m1, :].rearrange("p m t -> p (m t)"),
+                in_=x16[b, m0],
             )
-
-        score_bank = {}
 
         def score_pass(n, half, b):
             if b == 0:
                 score_bank[n, half] = psum.tile([P, 2, M_HALF], F32, name="bank")
             bank = score_bank[n, half]
             cols = slice(half * M_HALF, (half + 1) * M_HALF)
-            nc.tensor.matmul_mx(
-                out=bank[:, 0, :],
-                lhsT=w2_w[:, b, 2 * P * n : 2 * P * (n + 1)].bitcast(FP4X4),
-                lhsT_scale=w2_s[:, b, P * n : P * (n + 1)],
-                rhs=x_w[b][:, cols].bitcast(FP8X4),
-                rhs_scale=x_s[b][:, cols],
-                start=(b == 0),
-                stop=False,
-            )
             w_half, w_tile = divmod(n, N_TILES // 2)
             nc.tensor.matmul_mx(
                 out=bank[:, 1, :],
                 lhsT=w3_w[b, w_half][:, P * w_tile : P * (w_tile + 1)].bitcast(FP8X4),
                 lhsT_scale=w3_s[b, w_half][:, P * w_tile : P * (w_tile + 1)],
-                rhs=x_w[b][:, cols].bitcast(FP8X4),
+                rhs=x_w[b, half].bitcast(FP8X4),
+                rhs_scale=x_s[b][:, cols],
+                start=(b == 0),
+                stop=False,
+            )
+            nc.tensor.matmul_mx(
+                out=bank[:, 0, :],
+                lhsT=w2_w[:, b, 2 * P * n : 2 * P * (n + 1)].bitcast(FP4X4),
+                lhsT_scale=w2_s[:, b, P * n : P * (n + 1)],
+                rhs=x_w[b, half].bitcast(FP8X4),
                 rhs_scale=x_s[b][:, cols],
                 start=False,
                 stop=(b == H_PASSES - 1),
@@ -238,99 +310,133 @@ def tile_list_penstock_blister_scores_kernel(
             bank = score_bank[n, half]
             gated = silu_pool.tile([P, M_HALF], F32, name="gated")
             nc.scalar.activation(out=gated[:], in_=bank[:, 0, :], func=ACT.Silu)
-            result = held("result%d%d" % (n, half), [P, M_HALF], F32)
-            nc.vector.tensor_tensor(out=result[:], in0=bank[:, 1, :], in1=gated[:], op=ALU.add)
-            nc.sync.dma_start(out=out[P * n : P * (n + 1), half * M_HALF : (half + 1) * M_HALF], in_=result[:])
+            nc.vector.tensor_tensor(out=result[half][:, n, :], in0=bank[:, 1, :], in1=gated[:], op=ALU.add)
+            nc.sync.dma_start(
+                out=out[P * n : P * (n + 1), half * M_HALF : (half + 1) * M_HALF], in_=result[half][:, n, :]
+            )
 
-        def load_pair(i):
-            load_page(2 * i)
-            load_page(2 * i + 1)
-            load_gm(i)
+        def w1_low(c0, width, a0, a1):
+            round_w1_low(c0, width, a0, a1)
+            quantise_w1_low(c0, width, a0, a1)
 
-        def features(b):
-            for s in range(PACK * b, PACK * (b + 1)):
-                first_product(s)
-                tanh_of(s)
-                feature(s)
 
-        def rewrite_pair(i, m1):
-            for s in (2 * i, 2 * i + 1):
-                put(s)
-            for s in (2 * i, 2 * i + 1):
-                fetch_new(s, 0, m1)
-
-        for a in range(K_PASSES):
-            load_w1(a, 0)
+        load_w1_low(0, P, 0, 3)
         nc.sync.dma_start(idx[:], offs)
         for a in range(K_PASSES):
             load_tab(a)
         nc.sync.dma_start(idx4[:], offs4)
-        load_pair(0)
+        load_page(0)
+        load_gm_low(0)
         nc.sync.dma_start(idx2[:], offs2)
+        nc.sync.dma_start(out=wgs_low[:], in_=wgs)
+        load_w1_low(P, P, 0, 3)
+        load_page(1)
+        load_gm_low(1)
         nc.sync.dma_start(idx3[:], offs3)
-        load_wgs(0)
+        load_w1_low(2 * P, 2 * P, 0, 2)
+        load_w1_low(2 * P, 2 * P, 2, 3)
+        load_page(2)
+        load_gm_low(2)
+        load_w1_high(0)
+        load_w1_high(1)
+        load_page(3)
+        load_gm_low(3)
+        load_w1_high(2)
+        load_page(4)
+        load_page(5)
+        load_gm_high(0)
+        load_wgs_high(0)
 
-        for a in range(K_PASSES):
-            round_w1(a, 0)
-            quantise_w1(a, 0)
-        nc.vector.tensor_copy(out=v_s[:], in_=tab_s[:].indirect(idx[:]))
+        w1_low(0, P, 0, 3)
+        gather_scales()
         for a in range(K_PASSES):
             gather_words(a)
-        features(0)
         fetch_old(0)
+        feature(0)
+        put(0)
+        w1_low(P, P, 0, 3)
         fetch_old(1)
-
-        x32[0, 0] = held("x32_a", [P, PACK, M], F32)
-        x32[1, 0] = held("x32_b", [P, PACK, M_HALF], F32)
-        rewrite_pair(0, M)
-
-        for a in range(K_PASSES):
-            load_w1(a, 1)
-        load_pair(1)
-        load_wgs(1)
-        load_pair(2)
-        for a in range(K_PASSES):
-            round_w1(a, 1)
-            quantise_w1(a, 1)
+        fetch_new_low(0)
+        feature(1)
+        put(1)
+        w1_low(2 * P, 2 * P, 0, 2)
+        w1_low(2 * P, 2 * P, 2, 3)
         fetch_old(2)
+        fetch_new_low(1)
+        feature(2)
+        feature(3)
+        put(2)
+        for a in range(K_PASSES):
+            round_w1_high(a)
+            quantise_w1_high(a)
         fetch_old(3)
-        features(1)
-        rewrite_pair(1, M)
-        round_x(0, 0, M)
-
-        for b in range(H_PASSES):
-            for half in range(2):
-                load_w3(b, half)
-        nc.sync.dma_start(out=w2_w[:].bitcast(I32), in_=w2_words.rearrange("a p c -> p a c").bitcast(I32))
-        load_pair(3)
-
+        fetch_new_low(2)
+        put(3)
+        fetch_new_low(3)
         fetch_old(4)
         fetch_old(5)
-        rewrite_pair(2, M_HALF)
-        quantise_x(0, 0, M)
-        for b in range(H_PASSES):
-            for half in range(2):
-                round_w3(b, half)
-                quantise_w3(b, half)
-        for n in range(N_TILES):
-            score_pass(n, 0, 0)
-        fetch_old(6)
-        fetch_old(7)
-        rewrite_pair(3, M_HALF)
-
-        round_x(1, 0, M_HALF)
-        x32[1, M_HALF] = held("wgs1", [P, PACK, M_HALF], F32)
         for s in range(PACK, SLICES):
+            feature(s)
+        x_rows[0] = held("tab_w0", [P, M // P, PASS], BF16)
+        for s in range(PACK):
+            turn_x_low(s)
+        turn_x_back(0)
+        turn_x_back(1)
+        put(4)
+        put(5)
+        load_page(6)
+        load_gm_high(1)
+        fetch_old(6)
+        load_w2()
+        for b, half in ((0, 0), (1, 0), (1, 1), (0, 1)):
+            load_w3(b, half)
+            round_w3(b, half)
+            if (b, half) != (0, 1):
+                quantise_w3(b, half)
+        x_w[0, 0] = held("h_mid", [P, M_HALF], U32)[:]
+        quantise_x(0, 0, M_HALF)
+        for n in range(N_TILES // 2):
+            score_pass(n, 0, 0)
+        load_wgs_high(1)
+        load_page(7)
+        put(6)
+        fetch_old(7)
+        x32[1, 0] = held("gm_high1", [P, PACK, M_HALF], F32)[:]
+        for s in range(PACK, SLICES - 1):
+            fetch_new(s, 0, M_HALF)
+        put(7)
+
+        late_words = held("h_last", [P, N_HALF + M_HALF], U32)
+        w3_w[0, 1] = late_words[:, 0:N_HALF]
+        x_w[0, 1] = late_words[:, N_HALF : N_HALF + M_HALF]
+        for half in range(2):
+            x_w[1, half] = held("x_w1%d" % half, [P, M_HALF], U32)[:]
+        late = held("wgs_high1", [P, (PACK + 1) * M_HALF], F32)
+        x32[1, M_HALF] = late[:, 0 : PACK * M_HALF].rearrange("p (t m) -> p t m", t=PACK)
+        x16[1, 0] = late[:, (PACK - 1) * M_HALF : (PACK + 1) * M_HALF].bitcast(BF16)
+        quantise_w3(0, 1)
+        fetch_new(7, 0, M_HALF)
+        quantise_x(0, M_HALF, M)
+        round_x(1, 0, M_HALF, False)
+        for n in range(N_TILES // 2, N_TILES):
+            score_pass(n, 0, 0)
+        for n in range(2):
+            score_pass(n, 1, 0)
+        for s in range(PACK, SLICES - 1):
             fetch_new(s, M_HALF, M)
         quantise_x(1, 0, M_HALF)
-        round_x(1, M_HALF, M)
+        fetch_new(SLICES - 1, M_HALF, M)
+        round_x(1, M_HALF, M, True)
         for n in range(N_TILES):
             score_pass(n, 0, 1)
         quantise_x(1, M_HALF, M)
+        result[0] = held("tab_w1", [P, N_TILES, M_HALF], F32)
+        result[1] = held("tab_w2", [P, N_TILES, M_HALF], F32)
         for n in range(N_TILES):
             finish(n, 0)
         for n in range(N_TILES):
-            score_pass(n, 1, 0)
+            if n >= 2:
+                score_pass(n, 1, 0)
             score_pass(n, 1, 1)
         for n in range(N_TILES):
             finish(n, 1)

@@ -35,11 +35,11 @@ def tile_list_penstock_blister_scores_kernel(
     nc = tc.nc
     with ExitStack() as ctx:
         keep = ctx.enter_context(tc.tile_pool(name="keep", bufs=1))
-        raw_pool = ctx.enter_context(tc.tile_pool(name="raw", bufs=6))
+        raw_pool = ctx.enter_context(tc.tile_pool(name="raw", bufs=4))
         grouped_pool = ctx.enter_context(tc.tile_pool(name="grouped", bufs=4))
         tanh_pool = ctx.enter_context(tc.tile_pool(name="tanh", bufs=4))
-        h_pool = ctx.enter_context(tc.tile_pool(name="h", bufs=3))
-        old_pool = ctx.enter_context(tc.tile_pool(name="old", bufs=6))
+        h_pool = ctx.enter_context(tc.tile_pool(name="h", bufs=2))
+        old_pool = ctx.enter_context(tc.tile_pool(name="old", bufs=4))
         silu_pool = ctx.enter_context(tc.tile_pool(name="silu", bufs=4))
         psum = ctx.enter_context(tc.psum_pool(name="psum", bufs=8))
 
@@ -53,10 +53,10 @@ def tile_list_penstock_blister_scores_kernel(
         tab_w = [held("tab_w%d" % a, [P, T], U32) for a in range(K_PASSES)]
         tab_s = held("tab_s", [P, T], U8)
         v_w = [held("v_w%d" % a, [P, S], U32) for a in range(K_PASSES)]
-        v_s = held("v_s", [P, S], U8)
+        v_s = held("tab_w0", [P, S], U8)
         page = [held("page%d" % s, [P, T2], F32) for s in range(SLICES)]
-        gm_low = [held("gm_low%d" % s, [P, M], F32) for s in range(PACK)]
-        gm_high = [held("gm_high%d" % i, [P, 2, M], F32) for i in range(2)]
+        gm_low = [held("gm_low%d" % s, [P, M], F32) for s in range(SLICES - 2)]
+        gm_last = held("gm_last", [P, 2, M], F32)
         wgs_low = held("wgs_low", [P, S], F32)
         wgs_high = [held("wgs_high%d" % i, [P, 2, S], F32) for i in range(2)]
         d_sb = [held("d_sb%d" % b, [P, PACK], F32) for b in range(H_PASSES)]
@@ -65,6 +65,7 @@ def tile_list_penstock_blister_scores_kernel(
         x16 = {key: held("x16_%d%d" % key, [P, M_HALF * PACK], BF16)[:] for key in ((0, 0), (0, M_HALF), (1, M_HALF))}
         ident = held("ident", [P, P], F32)
         x_rows = {}
+        wgs_turned = {}
         x_s = [held("x_s%d" % b, [P, M], U8) for b in range(H_PASSES)]
         x_w = {}
         x_low = {}
@@ -82,29 +83,30 @@ def tile_list_penstock_blister_scores_kernel(
         score_bank = {}
 
         nc.vector.memset(tab_s[:].bitcast(I32), 0)
-        for q in range(P // QUAD):
-            nc.scalar.dma_start(
-                out=tab_s[QUAD * q : QUAD * q + 4 * K_PASSES, :].bitcast(I32),
-                in_=tab_scales[:, 4 * q : 4 * q + 4, :].bitcast(I32),
-            )
         warm = held("warm", [P, 2], F32)
         nc.vector.memset(warm[:, 0:1], 0.0)
         nc.scalar.activation(out=warm[:, 1:2], in_=warm[:, 0:1], func=ACT.Silu)
-        with nc.allow_non_contiguous_dma(reason="one value of d for each partition and slice"):
-            nc.gpsimd.dma_start(out=d_sb[0][:], in_=d[0:PASS].rearrange("(c p) -> p c", p=P))
-        nc.gpsimd.dma_start(out=d_sb[1][:], in_=d[PASS:H].rearrange("(p t) -> p t", t=PACK))
-        nc.gpsimd.memset(w2_s[:].rearrange("p a c -> p (a c)").bitcast(I32), 0)
+        d_rows = held("d_rows", [P, P], F32)
+        nc.vector.memset(d_rows[:], 0.0)
+        nc.vector.memset(w2_s[:].rearrange("p a c -> p (a c)").bitcast(I32), 0)
+        make_identity(nc, ident[:])
+        for q in range(P // QUAD):
+            nc.gpsimd.dma_start(
+                out=tab_s[QUAD * q : QUAD * q + 4 * K_PASSES, :].bitcast(I32),
+                in_=tab_scales[:, 4 * q : 4 * q + 4, :].bitcast(I32),
+            )
         for q in range(P // QUAD):
             nc.gpsimd.dma_start(
                 out=w2_s[QUAD * q : QUAD * q + 4, :, :].bitcast(I32),
                 in_=w2_scales[:, 4 * q : 4 * q + 4, :].rearrange("a q c -> q a c").bitcast(I32),
             )
 
-        make_identity(nc, ident[:])
-
         def load_w1_low(c0, width, a0, a1):
             key = ("low", c0, a0)
-            raw[key] = raw_pool.tile([P, a1 - a0, PACK, width], F32, name="raw")
+            if key == ("low", 2 * P, 0):
+                raw[key] = held("raw_mid", [P, a1 - a0, PACK, width], F32)
+            else:
+                raw[key] = raw_pool.tile([P, a1 - a0, PACK, width], F32, name="raw")
             for a in range(a0, a1):
                 rows = w1[a * PASS : (a + 1) * PASS, c0 : c0 + width]
                 nc.sync.dma_start(out=raw[key][:, a - a0, :, :], in_=rows.rearrange("(p j) c -> p j c", j=PACK))
@@ -114,10 +116,10 @@ def tile_list_penstock_blister_scores_kernel(
             rows = w1[a * PASS : (a + 1) * PASS, PASS:H]
             nc.sync.dma_start(out=raw["high", a][:], in_=rows.rearrange("(p j) c -> p j c", j=PACK))
 
-        def load_w3(b, half):
-            raw["w3", b, half] = raw_pool.tile([P, PACK, N_HALF], F32, name="raw")
-            rows = w3[b * PASS : (b + 1) * PASS, half * N_HALF : (half + 1) * N_HALF]
-            nc.sync.dma_start(out=raw["w3", b, half][:], in_=rows.rearrange("(p j) c -> p j c", j=PACK))
+        def load_w3(b):
+            raw["w3", b] = raw_pool.tile([P, PACK, N], F32, name="raw")
+            rows = w3[b * PASS : (b + 1) * PASS, :]
+            nc.sync.dma_start(out=raw["w3", b][:], in_=rows.rearrange("(p j) c -> p j c", j=PACK))
 
         def load_w2():
             nc.sync.dma_start(out=w2_w[:].bitcast(I32), in_=w2_words.rearrange("a p c -> p a c").bitcast(I32))
@@ -135,18 +137,15 @@ def tile_list_penstock_blister_scores_kernel(
             nc.sync.dma_start(out=page[s][:], in_=rows)
 
         def load_gm_low(s):
-            nc.sync.dma_start(out=gm_low[s][:], in_=gm[s * P : (s + 1) * P, :])
+            if s < PACK:
+                rows = gm[s * P : (s + 1) * P, :]
+            else:
+                rows = gm[PASS:H, :].rearrange("(p t) m -> p t m", t=PACK)[:, s - PACK, :]
+            nc.sync.dma_start(out=gm_low[s][:], in_=rows)
 
-        def load_gm_high(i):
+        def load_gm_last():
             rows = gm[PASS:H, :].rearrange("(p t) m -> p t m", t=PACK)
-            nc.sync.dma_start(out=gm_high[i][:], in_=rows[:, 2 * i : 2 * i + 2, :])
-
-        def load_wgs_high(i):
-            rows = wgs.rearrange("(q t) j -> q t j", t=PACK)
-            for q in (0, 2, 1, 3):
-                nc.sync.dma_start(
-                    out=wgs_high[i][QUAD * q : QUAD * (q + 1), :, :], in_=rows[:, 2 * i : 2 * i + 2, :]
-                )
+            nc.sync.dma_start(out=gm_last[:], in_=rows[:, 2:PACK, :])
 
         def round_w1_low(c0, width, a0, a1):
             key = ("low", c0, a0)
@@ -184,7 +183,7 @@ def tile_list_penstock_blister_scores_kernel(
             grouped["w3", b, half] = grouped_pool.tile([P, N_HALF * PACK], BF16, name="grouped", align_bytes=64)
             nc.scalar.copy(
                 out=grouped["w3", b, half][:].rearrange("p (c i j) -> p c j i", i=4, j=PACK),
-                in_=raw["w3", b, half][:].rearrange("p j (c i) -> p c j i", i=4),
+                in_=raw["w3", b][:, :, half * N_HALF : (half + 1) * N_HALF].rearrange("p j (c i) -> p c j i", i=4),
             )
 
         def quantise_w3(b, half):
@@ -220,9 +219,7 @@ def tile_list_penstock_blister_scores_kernel(
                 h[s] = held("h_last", [P, S], F32)
             elif s == PACK:
                 h[s] = held("h_mid", [P, S], F32)
-            elif s == 0:
-                h[s] = held("gm_low0", [P, S], F32)
-            else:
+            elif s > 1:
                 h[s] = h_pool.tile([P, S], F32, name="h")
             nc.vector.scalar_tensor_tensor(
                 out=h[s][:], in0=tanh_f[s][:], scalar=d_sb[s // PACK][:, s % PACK : s % PACK + 1], in1=f_bank[s][:], op0=ALU.mult, op1=ALU.max
@@ -230,7 +227,7 @@ def tile_list_penstock_blister_scores_kernel(
 
         def fetch_old(s):
             old[s] = old_pool.tile([P, M], F32, name="old")
-            factor = gm_low[s][:] if s < PACK else gm_high[(s - PACK) // 2][:, s % 2, :]
+            factor = gm_low[s][:] if s < SLICES - 2 else gm_last[:, s % 2, :]
             nc.vector.tensor_tensor(out=old[s][:], in0=page[s][:].indirect(idx4[:]), in1=factor, op=ALU.mult)
 
         def put(s):
@@ -238,8 +235,25 @@ def tile_list_penstock_blister_scores_kernel(
             nc.vector.tensor_tensor(out=page[s][:].indirect(idx2[:]), in0=h[s][:], in1=factor, op=ALU.mult)
 
         def fetch_new_low(s):
-            x_low[s] = held("gm_low%d" % ((s + 1) % PACK), [P, M], F32)
             nc.vector.tensor_tensor(out=x_low[s][:], in0=page[s][:].indirect(idx3[:]), in1=old[s][:], op=ALU.add)
+
+        def turn_wgs():
+            bank = psum.tile([P, S // P, P], F32, name="bank")
+            for c in range(S // P):
+                nc.tensor.transpose(bank[:, c, :], wgs_low[:, c * P : (c + 1) * P], ident[:])
+            wgs_turned[0] = held("raw_mid", [P, PACK, S // P, P // QUAD, QUAD], F32)
+            for g in range(P // QUAD):
+                nc.scalar.copy(
+                    out=wgs_turned[0][:, :, :, g, :], in_=bank[:].rearrange("p c (q t) -> p t c q", t=PACK)
+                )
+
+        def deal_wgs(t):
+            bank = psum.tile([P, S // P, P], F32, name="bank")
+            for c in range(S // P):
+                nc.tensor.transpose(
+                    bank[:, c, :], wgs_turned[0][:, t, c, :, :].rearrange("p g q -> p (g q)"), ident[:]
+                )
+            nc.scalar.copy(out=wgs_high[t // 2][:, t % 2, :], in_=bank[:].rearrange("p c j -> p (c j)"))
 
         def turn_x_low(s):
             bank = psum.tile([P, PACK, P], F32, name="bank")
@@ -320,8 +334,10 @@ def tile_list_penstock_blister_scores_kernel(
             quantise_w1_low(c0, width, a0, a1)
 
 
-        load_w1_low(0, P, 0, 3)
+        load_w1_low(0, 2 * P, 0, 2)
+        load_w1_low(0, 2 * P, 2, 3)
         nc.sync.dma_start(idx[:], offs)
+        nc.sync.dma_start(out=d_rows[0:PACK, :], in_=d[0:PASS].rearrange("(c p) -> c p", p=P))
         for a in range(K_PASSES):
             load_tab(a)
         nc.sync.dma_start(idx4[:], offs4)
@@ -329,7 +345,6 @@ def tile_list_penstock_blister_scores_kernel(
         load_gm_low(0)
         nc.sync.dma_start(idx2[:], offs2)
         nc.sync.dma_start(out=wgs_low[:], in_=wgs)
-        load_w1_low(P, P, 0, 3)
         load_page(1)
         load_gm_low(1)
         nc.sync.dma_start(idx3[:], offs3)
@@ -337,71 +352,85 @@ def tile_list_penstock_blister_scores_kernel(
         load_w1_low(2 * P, 2 * P, 2, 3)
         load_page(2)
         load_gm_low(2)
+        nc.sync.dma_start(out=d_sb[1][:], in_=d[PASS:H].rearrange("(p t) -> p t", t=PACK))
+
+        w1_low(0, 2 * P, 0, 2)
+        w1_low(0, 2 * P, 2, 3)
+        d_bank = psum.tile([P, P], F32, name="bank")
+        nc.tensor.transpose(d_bank[:], d_rows[:], ident[:])
+        nc.vector.tensor_copy(out=d_sb[0][:], in_=d_bank[:, 0:PACK])
+        gather_words(0)
+        gather_scales()
+        for a in range(1, K_PASSES):
+            gather_words(a)
+        fetch_old(0)
+        h_first = held("gm_low0", [P, 2, S], F32)
+        for s in range(2):
+            h[s] = h_first[:, s, :]
+            feature(s)
+        put(0)
+        fetch_old(1)
+        put(1)
+        w1_low(2 * P, 2 * P, 0, 2)
+        w1_low(2 * P, 2 * P, 2, 3)
         load_w1_high(0)
         load_w1_high(1)
         load_page(3)
         load_gm_low(3)
         load_w1_high(2)
         load_page(4)
+        load_gm_low(4)
+        load_gm_low(5)
         load_page(5)
-        load_gm_high(0)
-        load_wgs_high(0)
-
-        w1_low(0, P, 0, 3)
-        gather_scales()
-        for a in range(K_PASSES):
-            gather_words(a)
-        fetch_old(0)
-        feature(0)
-        put(0)
-        w1_low(P, P, 0, 3)
-        fetch_old(1)
-        fetch_new_low(0)
-        feature(1)
-        put(1)
-        w1_low(2 * P, 2 * P, 0, 2)
-        w1_low(2 * P, 2 * P, 2, 3)
         fetch_old(2)
-        fetch_new_low(1)
+        x_first = held("gm_low2", [P, 2, M], F32)
+        for s in range(2):
+            x_low[s] = x_first[:, s, :]
+            fetch_new_low(s)
+        turn_wgs()
         feature(2)
         feature(3)
         put(2)
         for a in range(K_PASSES):
             round_w1_high(a)
             quantise_w1_high(a)
+        for t in range(PACK):
+            deal_wgs(t)
         fetch_old(3)
-        fetch_new_low(2)
         put(3)
-        fetch_new_low(3)
         fetch_old(4)
+        x_second = held("gm_low4", [P, 2, M], F32)
+        for s in range(2, PACK):
+            x_low[s] = x_second[:, s - 2, :]
+            fetch_new_low(s)
         fetch_old(5)
         for s in range(PACK, SLICES):
             feature(s)
+        put(4)
+        put(5)
+        load_w2()
+        load_w3(0)
+        load_w3(1)
+        load_page(6)
+        load_gm_last()
+        load_page(7)
+        for b, half in ((0, 0), (0, 1), (1, 0), (1, 1)):
+            round_w3(b, half)
+            if (b, half) != (0, 1):
+                quantise_w3(b, half)
         x_rows[0] = held("tab_w0", [P, M // P, PASS], BF16)
         for s in range(PACK):
             turn_x_low(s)
         turn_x_back(0)
         turn_x_back(1)
-        put(4)
-        put(5)
-        load_page(6)
-        load_gm_high(1)
         fetch_old(6)
-        load_w2()
-        for b, half in ((0, 0), (1, 0), (1, 1), (0, 1)):
-            load_w3(b, half)
-            round_w3(b, half)
-            if (b, half) != (0, 1):
-                quantise_w3(b, half)
+        put(6)
         x_w[0, 0] = held("h_mid", [P, M_HALF], U32)[:]
         quantise_x(0, 0, M_HALF)
         for n in range(N_TILES // 2):
             score_pass(n, 0, 0)
-        load_wgs_high(1)
-        load_page(7)
-        put(6)
         fetch_old(7)
-        x32[1, 0] = held("gm_high1", [P, PACK, M_HALF], F32)[:]
+        x32[1, 0] = held("gm_last", [P, PACK, M_HALF], F32)[:]
         for s in range(PACK, SLICES - 1):
             fetch_new(s, 0, M_HALF)
         put(7)

@@ -27,6 +27,7 @@ SLICES = H_PASSES * PACK
 N_TILES = N // P
 N_HALF = N // 2
 M_HALF = M // 2
+TURNED = (6, 7)
 
 
 def tile_list_penstock_blister_scores_kernel(
@@ -35,10 +36,11 @@ def tile_list_penstock_blister_scores_kernel(
     nc = tc.nc
     with ExitStack() as ctx:
         keep = ctx.enter_context(tc.tile_pool(name="keep", bufs=1))
-        raw_pool = ctx.enter_context(tc.tile_pool(name="raw", bufs=4))
+        raw_pool = ctx.enter_context(tc.tile_pool(name="raw", bufs=3))
         grouped_pool = ctx.enter_context(tc.tile_pool(name="grouped", bufs=4))
         tanh_pool = ctx.enter_context(tc.tile_pool(name="tanh", bufs=4))
         h_pool = ctx.enter_context(tc.tile_pool(name="h", bufs=2))
+        turn_pool = ctx.enter_context(tc.tile_pool(name="turn", bufs=4))
         old_pool = ctx.enter_context(tc.tile_pool(name="old", bufs=4))
         silu_pool = ctx.enter_context(tc.tile_pool(name="silu", bufs=4))
         psum = ctx.enter_context(tc.psum_pool(name="psum", bufs=8))
@@ -62,7 +64,7 @@ def tile_list_penstock_blister_scores_kernel(
         d_sb = [held("d_sb%d" % b, [P, PACK], F32) for b in range(H_PASSES)]
         w2_w = held("w2_w", [P, H_PASSES, 2 * N], U8)
         w2_s = held("w2_s", [P, H_PASSES, N], U8)
-        x16 = {key: held("x16_%d%d" % key, [P, M_HALF * PACK], BF16)[:] for key in ((0, 0), (0, M_HALF), (1, M_HALF))}
+        x16 = {key: held("x16_%d%d" % key, [P, M_HALF * PACK], BF16)[:] for key in ((0, 0), (0, M_HALF))}
         ident = held("ident", [P, P], F32)
         x_rows = {}
         wgs_turned = {}
@@ -215,6 +217,8 @@ def tile_list_penstock_blister_scores_kernel(
                 )
             tanh_f[s] = tanh_pool.tile([P, S], F32, name="tanh_f")
             nc.scalar.activation(out=tanh_f[s][:], in_=f_bank[s][:], func=ACT.Tanh)
+            if s in TURNED:
+                return
             if s == SLICES - 1:
                 h[s] = held("h_last", [P, S], F32)
             elif s == PACK:
@@ -224,6 +228,34 @@ def tile_list_penstock_blister_scores_kernel(
             nc.vector.scalar_tensor_tensor(
                 out=h[s][:], in0=tanh_f[s][:], scalar=d_sb[s // PACK][:, s % PACK : s % PACK + 1], in1=f_bank[s][:], op0=ALU.mult, op1=ALU.max
             )
+
+        def add_turned(bank, first, second):
+            for c in range(S // P):
+                cols = slice(c * P, (c + 1) * P)
+                nc.tensor.matmul(bank[:, cols], first[:, cols], ident[:], start=True, stop=False, is_transpose=True)
+                nc.tensor.matmul(bank[:, cols], second[:, cols], ident[:], start=False, stop=True, is_transpose=True)
+
+        def feature_by_turns(s, name):
+            scaled = turn_pool.tile([P, S], F32, name="turn")
+            nc.scalar.activation(
+                out=scaled[:], in_=tanh_f[s][:], func=ACT.Copy, scale=d_sb[s // PACK][:, s % PACK : s % PACK + 1]
+            )
+            minus_f = turn_pool.tile([P, S], F32, name="turn")
+            nc.scalar.activation(out=minus_f[:], in_=f_bank[s][:], func=ACT.Copy, scale=-1.0)
+            gap_bank = psum.tile([P, S], F32, name="bank")
+            add_turned(gap_bank, scaled, minus_f)
+            f_turned_bank = psum.tile([P, S], F32, name="bank")
+            for c in range(S // P):
+                cols = slice(c * P, (c + 1) * P)
+                nc.tensor.transpose(f_turned_bank[:, cols], minus_f[:, cols], ident[:])
+            f_turned = turn_pool.tile([P, S], F32, name="turn")
+            nc.scalar.activation(out=f_turned[:], in_=f_turned_bank[:], func=ACT.Copy, scale=-1.0)
+            gap = turn_pool.tile([P, S], F32, name="turn")
+            nc.scalar.activation(out=gap[:], in_=gap_bank[:], func=ACT.Relu)
+            h_bank = psum.tile([P, S], F32, name="bank")
+            add_turned(h_bank, f_turned, gap)
+            h[s] = held(name, [P, S], F32)
+            nc.scalar.copy(out=h[s][:], in_=h_bank[:])
 
         def fetch_old(s):
             old[s] = old_pool.tile([P, M], F32, name="old")
@@ -322,7 +354,10 @@ def tile_list_penstock_blister_scores_kernel(
 
         def finish(n, half):
             bank = score_bank[n, half]
-            gated = silu_pool.tile([P, M_HALF], F32, name="gated")
+            if (n, half) == (0, 0):
+                gated = held("gated_first", [P, M_HALF], F32)
+            else:
+                gated = silu_pool.tile([P, M_HALF], F32, name="gated")
             nc.scalar.activation(out=gated[:], in_=bank[:, 0, :], func=ACT.Silu)
             nc.vector.tensor_tensor(out=result[half][:, n, :], in0=bank[:, 1, :], in1=gated[:], op=ALU.add)
             nc.sync.dma_start(
@@ -373,10 +408,10 @@ def tile_list_penstock_blister_scores_kernel(
         put(1)
         w1_low(2 * P, 2 * P, 0, 2)
         w1_low(2 * P, 2 * P, 2, 3)
-        load_w1_high(0)
-        load_w1_high(1)
         load_page(3)
         load_gm_low(3)
+        load_w1_high(0)
+        load_w1_high(1)
         load_w1_high(2)
         load_page(4)
         load_gm_low(4)
@@ -387,6 +422,7 @@ def tile_list_penstock_blister_scores_kernel(
         for s in range(2):
             x_low[s] = x_first[:, s, :]
             fetch_new_low(s)
+        fetch_old(3)
         turn_wgs()
         feature(2)
         feature(3)
@@ -396,7 +432,9 @@ def tile_list_penstock_blister_scores_kernel(
             quantise_w1_high(a)
         for t in range(PACK):
             deal_wgs(t)
-        fetch_old(3)
+        x_rows[0] = held("tab_w2", [P, M // P, PASS], BF16)
+        turn_x_low(0)
+        turn_x_low(1)
         put(3)
         fetch_old(4)
         x_second = held("gm_low4", [P, 2, M], F32)
@@ -406,24 +444,25 @@ def tile_list_penstock_blister_scores_kernel(
         fetch_old(5)
         for s in range(PACK, SLICES):
             feature(s)
+        feature_by_turns(6, "gm_low3")
+        turn_x_low(2)
+        turn_x_low(3)
+        feature_by_turns(7, "h_last")
+        turn_x_back(0)
+        turn_x_back(1)
         put(4)
+        load_page(6)
+        load_gm_last()
+        fetch_old(6)
         put(5)
         load_w2()
         load_w3(0)
         load_w3(1)
-        load_page(6)
-        load_gm_last()
         load_page(7)
         for b, half in ((0, 0), (0, 1), (1, 0), (1, 1)):
             round_w3(b, half)
             if (b, half) != (0, 1):
                 quantise_w3(b, half)
-        x_rows[0] = held("tab_w0", [P, M // P, PASS], BF16)
-        for s in range(PACK):
-            turn_x_low(s)
-        turn_x_back(0)
-        turn_x_back(1)
-        fetch_old(6)
         put(6)
         x_w[0, 0] = held("h_mid", [P, M_HALF], U32)[:]
         quantise_x(0, 0, M_HALF)
@@ -440,9 +479,9 @@ def tile_list_penstock_blister_scores_kernel(
         x_w[0, 1] = late_words[:, N_HALF : N_HALF + M_HALF]
         for half in range(2):
             x_w[1, half] = held("x_w1%d" % half, [P, M_HALF], U32)[:]
-        late = held("wgs_high1", [P, (PACK + 1) * M_HALF], F32)
+        late = held("wgs_high1", [P, PACK * M_HALF], F32)
         x32[1, M_HALF] = late[:, 0 : PACK * M_HALF].rearrange("p (t m) -> p t m", t=PACK)
-        x16[1, 0] = late[:, (PACK - 1) * M_HALF : (PACK + 1) * M_HALF].bitcast(BF16)
+        x16[1, 0] = late[:, 2 * M_HALF : PACK * M_HALF].bitcast(BF16)
         quantise_w3(0, 1)
         fetch_new(7, 0, M_HALF)
         quantise_x(0, M_HALF, M)
@@ -451,17 +490,20 @@ def tile_list_penstock_blister_scores_kernel(
             score_pass(n, 0, 0)
         for n in range(2):
             score_pass(n, 1, 0)
-        for s in range(PACK, SLICES - 1):
+        for s in range(PACK, SLICES - 2):
             fetch_new(s, M_HALF, M)
         quantise_x(1, 0, M_HALF)
-        fetch_new(SLICES - 1, M_HALF, M)
-        round_x(1, M_HALF, M, True)
+        for s in range(SLICES - 2, SLICES):
+            fetch_new(s, M_HALF, M)
         for n in range(N_TILES):
             score_pass(n, 0, 1)
-        quantise_x(1, M_HALF, M)
         result[0] = held("tab_w1", [P, N_TILES, M_HALF], F32)
         result[1] = held("tab_w2", [P, N_TILES, M_HALF], F32)
-        for n in range(N_TILES):
+        finish(0, 0)
+        x16[1, M_HALF] = held("gated_first", [P, M_HALF * PACK], BF16)[:]
+        round_x(1, M_HALF, M, True)
+        quantise_x(1, M_HALF, M)
+        for n in range(1, N_TILES):
             finish(n, 0)
         for n in range(N_TILES):
             if n >= 2:

from contextlib import ExitStack

import concourse.mybir as mybir
from concourse.masks import make_identity

K, H, N, T, S, T2, M = 1536, 1024, 768, 2048, 512, 1024, 512
FLOPS = 2 * K * H * S + 2 * 2 * H * N * M

F32 = mybir.dt.float32
BF16 = mybir.dt.bfloat16
I32 = mybir.dt.int32
U32 = mybir.dt.uint32
U16 = mybir.dt.uint16
U8 = mybir.dt.uint8
FP8X4 = mybir.dt.float8_e4m3fn_x4
FP4X4 = mybir.dt.float4_e2m1fn_x4
ACT = mybir.ActivationFunctionType
ALU = mybir.AluOpType

P = 128
PACK = 4
PASS = P * PACK
QUAD = 32
K_PASSES = K // PASS
H_PASSES = H // PASS
SLICES = H_PASSES * PACK
N_TILES = N // P
N_HALF = N // 2
M_HALF = M // 2
TURNED = (6, 7)


def tile_list_penstock_blister_scores_kernel(
    tc, tab_words, tab_scales, offs, offs2, offs3, offs4, w1, d, wgs, page0, gm, w2_words, w2_scales, w3, out
):
    nc = tc.nc
    with ExitStack() as ctx:
        keep = ctx.enter_context(tc.tile_pool(name="keep", bufs=1))
        raw_pool = ctx.enter_context(tc.tile_pool(name="raw", bufs=3))
        grouped_pool = ctx.enter_context(tc.tile_pool(name="grouped", bufs=4))
        tanh_pool = ctx.enter_context(tc.tile_pool(name="tanh", bufs=4))
        h_pool = ctx.enter_context(tc.tile_pool(name="h", bufs=2))
        turn_pool = ctx.enter_context(tc.tile_pool(name="turn", bufs=4))
        old_pool = ctx.enter_context(tc.tile_pool(name="old", bufs=4))
        silu_pool = ctx.enter_context(tc.tile_pool(name="silu", bufs=4))
        psum = ctx.enter_context(tc.psum_pool(name="psum", bufs=8))

        def held(name, shape, dtype):
            return keep.tile(shape, dtype, name=name, align_bytes=64)

        idx = held("idx", [P, S // 16], U16)
        idx2 = held("idx2", [P, S // 16], U16)
        idx3 = held("idx3", [P, M // 16], U16)
        idx4 = held("idx4", [P, M // 16], U16)
        tab_w = [held("tab_w%d" % a, [P, T], U32) for a in range(K_PASSES)]
        tab_s = held("tab_s", [P, T], U8)
        v_w = [held("v_w%d" % a, [P, S], U32) for a in range(K_PASSES)]
        v_s = held("tab_w0", [P, S], U8)
        page = [held("page%d" % s, [P, T2], F32) for s in range(SLICES)]
        gm_low = [held("gm_low%d" % s, [P, M], F32) for s in range(SLICES - 2)]
        gm_last = held("gm_last", [P, 2, M], F32)
        wgs_low = held("wgs_low", [P, S], F32)
        wgs_high = [held("wgs_high%d" % i, [P, 2, S], F32) for i in range(2)]
        d_sb = [held("d_sb%d" % b, [P, PACK], F32) for b in range(H_PASSES)]
        w2_w = held("w2_w", [P, H_PASSES, 2 * N], U8)
        w2_s = held("w2_s", [P, H_PASSES, N], U8)
        x16 = {key: held("x16_%d%d" % key, [P, M_HALF * PACK], BF16)[:] for key in ((0, 0), (0, M_HALF))}
        ident = held("ident", [P, P], F32)
        x_rows = {}
        wgs_turned = {}
        x_s = [held("x_s%d" % b, [P, M], U8) for b in range(H_PASSES)]
        x_w = {}
        x_low = {}
        x32 = {}
        w1_ops = {}
        w3_w = {}
        w3_s = {}
        raw = {}
        grouped = {}
        f_bank = {}
        tanh_f = {}
        h = {}
        old = {}
        result = {}
        score_bank = {}

        nc.vector.memset(tab_s[:].bitcast(I32), 0)
        warm = held("warm", [P, 2], F32)
        nc.vector.memset(warm[:, 0:1], 0.0)
        nc.scalar.activation(out=warm[:, 1:2], in_=warm[:, 0:1], func=ACT.Silu)
        d_rows = held("d_rows", [P, P], F32)
        nc.vector.memset(d_rows[:], 0.0)
        nc.vector.memset(w2_s[:].rearrange("p a c -> p (a c)").bitcast(I32), 0)
        make_identity(nc, ident[:])
        for q in range(P // QUAD):
            nc.gpsimd.dma_start(
                out=tab_s[QUAD * q : QUAD * q + 4 * K_PASSES, :].bitcast(I32),
                in_=tab_scales[:, 4 * q : 4 * q + 4, :].bitcast(I32),
            )
        for q in range(P // QUAD):
            nc.gpsimd.dma_start(
                out=w2_s[QUAD * q : QUAD * q + 4, :, :].bitcast(I32),
                in_=w2_scales[:, 4 * q : 4 * q + 4, :].rearrange("a q c -> q a c").bitcast(I32),
            )

        def load_w1_low(c0, width, a0, a1):
            key = ("low", c0, a0)
            if key == ("low", 2 * P, 0):
                raw[key] = held("raw_mid", [P, a1 - a0, PACK, width], F32)
            else:
                raw[key] = raw_pool.tile([P, a1 - a0, PACK, width], F32, name="raw")
            for a in range(a0, a1):
                rows = w1[a * PASS : (a + 1) * PASS, c0 : c0 + width]
                nc.sync.dma_start(out=raw[key][:, a - a0, :, :], in_=rows.rearrange("(p j) c -> p j c", j=PACK))

        def load_w1_high(a):
            raw["high", a] = raw_pool.tile([P, PACK, PASS], F32, name="raw")
            rows = w1[a * PASS : (a + 1) * PASS, PASS:H]
            nc.sync.dma_start(out=raw["high", a][:], in_=rows.rearrange("(p j) c -> p j c", j=PACK))

        def load_w3(b):
            raw["w3", b] = raw_pool.tile([P, PACK, N], F32, name="raw")
            rows = w3[b * PASS : (b + 1) * PASS, :]
            nc.sync.dma_start(out=raw["w3", b][:], in_=rows.rearrange("(p j) c -> p j c", j=PACK))

        def load_w2():
            nc.sync.dma_start(out=w2_w[:].bitcast(I32), in_=w2_words.rearrange("a p c -> p a c").bitcast(I32))

        def load_tab(a):
            nc.sync.dma_start(
                out=tab_w[a][:].bitcast(I32), in_=tab_words[a].rearrange("p t i -> p (t i)").bitcast(I32)
            )

        def load_page(s):
            if s < PACK:
                rows = page0[s * P : (s + 1) * P, :]
            else:
                rows = page0[PASS:H, :].rearrange("(p t) c -> p t c", t=PACK)[:, s - PACK, :]
            nc.sync.dma_start(out=page[s][:], in_=rows)

        def load_gm_low(s):
            if s < PACK:
                rows = gm[s * P : (s + 1) * P, :]
            else:
                rows = gm[PASS:H, :].rearrange("(p t) m -> p t m", t=PACK)[:, s - PACK, :]
            nc.sync.dma_start(out=gm_low[s][:], in_=rows)

        def load_gm_last():
            rows = gm[PASS:H, :].rearrange("(p t) m -> p t m", t=PACK)
            nc.sync.dma_start(out=gm_last[:], in_=rows[:, 2:PACK, :])

        def round_w1_low(c0, width, a0, a1):
            key = ("low", c0, a0)
            grouped[key] = grouped_pool.tile([P, (a1 - a0) * width * PACK], BF16, name="grouped", align_bytes=64)
            nc.scalar.copy(
                out=grouped[key][:].rearrange("p (a c i j) -> p a c j i", a=a1 - a0, i=4, j=PACK),
                in_=raw[key][:].rearrange("p a j (c i) -> p a c j i", i=4),
            )

        def quantise_w1_low(c0, width, a0, a1):
            key = ("low", c0, a0)
            words = held("w1_w%d_%d" % (c0, a0), [P, (a1 - a0) * width], U32)
            scales = held("w1_s%d_%d" % (c0, a0), [P, (a1 - a0) * width], U8)
            nc.vector.quantize_mx(out=words[:].bitcast(FP8X4), scales=scales[:], in_=grouped[key][:])
            for a in range(a0, a1):
                for c in range(width // P):
                    cols = slice((a - a0) * width + c * P, (a - a0) * width + (c + 1) * P)
                    w1_ops[c0 // P + c, a] = (words[:, cols], scales[:, cols])

        def round_w1_high(a):
            grouped["high", a] = grouped_pool.tile([P, PASS * PACK], BF16, name="grouped", align_bytes=64)
            nc.scalar.copy(
                out=grouped["high", a][:].rearrange("p (t m j) -> p m j t", t=PACK, j=PACK),
                in_=raw["high", a][:].rearrange("p j (m t) -> p m j t", t=PACK),
            )

        def quantise_w1_high(a):
            words = held("w1_high_w%d" % a, [P, PASS], U32)
            scales = held("w1_high_s%d" % a, [P, PASS], U8)
            nc.vector.quantize_mx(out=words[:].bitcast(FP8X4), scales=scales[:], in_=grouped["high", a][:])
            for t in range(PACK):
                w1_ops[PACK + t, a] = (words[:, t * P : (t + 1) * P], scales[:, t * P : (t + 1) * P])

        def round_w3(b, half):
            grouped["w3", b, half] = grouped_pool.tile([P, N_HALF * PACK], BF16, name="grouped", align_bytes=64)
            nc.scalar.copy(
                out=grouped["w3", b, half][:].rearrange("p (c i j) -> p c j i", i=4, j=PACK),
                in_=raw["w3", b][:, :, half * N_HALF : (half + 1) * N_HALF].rearrange("p j (c i) -> p c j i", i=4),
            )

        def quantise_w3(b, half):
            if (b, half) not in w3_w:
                w3_w[b, half] = held("w3_w%d%d" % (b, half), [P, N_HALF], U32)[:]
            w3_s[b, half] = held("w3_s%d%d" % (b, half), [P, N_HALF], U8)
            nc.vector.quantize_mx(
                out=w3_w[b, half].bitcast(FP8X4), scales=w3_s[b, half][:], in_=grouped["w3", b, half][:]
            )

        def gather_scales():
            nc.vector.tensor_copy(out=v_s[:], in_=tab_s[:].indirect(idx[:]))

        def gather_words(a):
            nc.vector.tensor_copy(out=v_w[a][:], in_=tab_w[a][:].indirect(idx[:]))

        def feature(s):
            f_bank[s] = psum.tile([P, S], F32, name="bank")
            for a in range(K_PASSES):
                words, scales = w1_ops[s, a]
                nc.tensor.matmul_mx(
                    out=f_bank[s][:],
                    lhsT=words.bitcast(FP8X4),
                    lhsT_scale=scales,
                    rhs=v_w[a][:].bitcast(FP8X4),
                    rhs_scale=v_s[4 * a : P, :],
                    start=(a == 0),
                    stop=(a == K_PASSES - 1),
                )
            tanh_f[s] = tanh_pool.tile([P, S], F32, name="tanh_f")
            nc.scalar.activation(out=tanh_f[s][:], in_=f_bank[s][:], func=ACT.Tanh)
            if s in TURNED:
                return
            if s == SLICES - 1:
                h[s] = held("h_last", [P, S], F32)
            elif s == PACK:
                h[s] = held("h_mid", [P, S], F32)
            elif s > 1:
                h[s] = h_pool.tile([P, S], F32, name="h")
            nc.vector.scalar_tensor_tensor(
                out=h[s][:], in0=tanh_f[s][:], scalar=d_sb[s // PACK][:, s % PACK : s % PACK + 1], in1=f_bank[s][:], op0=ALU.mult, op1=ALU.max
            )

        def add_turned(bank, first, second):
            for c in range(S // P):
                cols = slice(c * P, (c + 1) * P)
                nc.tensor.matmul(bank[:, cols], first[:, cols], ident[:], start=True, stop=False, is_transpose=True)
                nc.tensor.matmul(bank[:, cols], second[:, cols], ident[:], start=False, stop=True, is_transpose=True)

        def feature_by_turns(s, name):
            scaled = turn_pool.tile([P, S], F32, name="turn")
            nc.scalar.activation(
                out=scaled[:], in_=tanh_f[s][:], func=ACT.Copy, scale=d_sb[s // PACK][:, s % PACK : s % PACK + 1]
            )
            minus_f = turn_pool.tile([P, S], F32, name="turn")
            nc.scalar.activation(out=minus_f[:], in_=f_bank[s][:], func=ACT.Copy, scale=-1.0)
            gap_bank = psum.tile([P, S], F32, name="bank")
            add_turned(gap_bank, scaled, minus_f)
            f_turned_bank = psum.tile([P, S], F32, name="bank")
            for c in range(S // P):
                cols = slice(c * P, (c + 1) * P)
                nc.tensor.transpose(f_turned_bank[:, cols], minus_f[:, cols], ident[:])
            f_turned = turn_pool.tile([P, S], F32, name="turn")
            nc.scalar.activation(out=f_turned[:], in_=f_turned_bank[:], func=ACT.Copy, scale=-1.0)
            gap = turn_pool.tile([P, S], F32, name="turn")
            nc.scalar.activation(out=gap[:], in_=gap_bank[:], func=ACT.Relu)
            h_bank = psum.tile([P, S], F32, name="bank")
            add_turned(h_bank, f_turned, gap)
            h[s] = held(name, [P, S], F32)
            nc.scalar.copy(out=h[s][:], in_=h_bank[:])

        def fetch_old(s):
            old[s] = old_pool.tile([P, M], F32, name="old")
            factor = gm_low[s][:] if s < SLICES - 2 else gm_last[:, s % 2, :]
            nc.vector.tensor_tensor(out=old[s][:], in0=page[s][:].indirect(idx4[:]), in1=factor, op=ALU.mult)

        def put(s):
            factor = wgs_low[:] if s < PACK else wgs_high[(s - PACK) // 2][:, s % 2, :]
            nc.vector.tensor_tensor(out=page[s][:].indirect(idx2[:]), in0=h[s][:], in1=factor, op=ALU.mult)

        def fetch_new_low(s):
            nc.vector.tensor_tensor(out=x_low[s][:], in0=page[s][:].indirect(idx3[:]), in1=old[s][:], op=ALU.add)

        def turn_wgs():
            bank = psum.tile([P, S // P, P], F32, name="bank")
            for c in range(S // P):
                nc.tensor.transpose(bank[:, c, :], wgs_low[:, c * P : (c + 1) * P], ident[:])
            wgs_turned[0] = held("raw_mid", [P, PACK, S // P, P // QUAD, QUAD], F32)
            for g in range(P // QUAD):
                nc.scalar.copy(
                    out=wgs_turned[0][:, :, :, g, :], in_=bank[:].rearrange("p c (q t) -> p t c q", t=PACK)
                )

        def deal_wgs(t):
            bank = psum.tile([P, S // P, P], F32, name="bank")
            for c in range(S // P):
                nc.tensor.transpose(
                    bank[:, c, :], wgs_turned[0][:, t, c, :, :].rearrange("p g q -> p (g q)"), ident[:]
                )
            nc.scalar.copy(out=wgs_high[t // 2][:, t % 2, :], in_=bank[:].rearrange("p c j -> p (c j)"))

        def turn_x_low(s):
            bank = psum.tile([P, PACK, P], F32, name="bank")
            for c in range(M // P):
                nc.tensor.transpose(bank[:, c, :], x_low[s][:, c * P : (c + 1) * P], ident[:])
            nc.scalar.copy(out=x_rows[0][:, :, s * P : (s + 1) * P], in_=bank[:])

        def turn_x_back(i):
            bank = psum.tile([P, 2, 2, P], F32, name="bank")
            for c in range(2):
                words = x_rows[0][:, 2 * i + c, :].bitcast(F32)
                for u in range(2):
                    nc.tensor.transpose(bank[:, c, u, :], words[:, u : PASS // 2 : 2], ident[:])
            half = x16[0, i * M_HALF].bitcast(F32)
            nc.scalar.copy(
                out=half.rearrange("p (c m u) -> p c m u", c=2, u=2), in_=bank[:].rearrange("p c u m -> p c m u")
            )

        def fetch_new(s, m0, m1):
            nc.vector.tensor_tensor(
                out=x32[1, m0][:, s - PACK, :],
                in0=page[s][:].indirect(idx3[:, m0 // 16 : m1 // 16]),
                in1=old[s][:, m0:m1],
                op=ALU.add,
            )

        def round_x(b, m0, m1, on_vector):
            dst = x16[b, m0].rearrange("p (c i t) -> p c t i", i=4, t=PACK)
            src = x32[b, m0].rearrange("p t (c i) -> p c t i", i=4)
            if on_vector:
                nc.vector.tensor_copy(out=dst, in_=src)
            else:
                nc.scalar.copy(out=dst, in_=src)

        def quantise_x(b, m0, m1):
            nc.vector.quantize_mx(
                out=x_w[b, m0 // M_HALF].bitcast(FP8X4),
                scales=x_s[b][:, m0:m1],
                in_=x16[b, m0],
            )

        def score_pass(n, half, b):
            if b == 0:
                score_bank[n, half] = psum.tile([P, 2, M_HALF], F32, name="bank")
            bank = score_bank[n, half]
            cols = slice(half * M_HALF, (half + 1) * M_HALF)
            w_half, w_tile = divmod(n, N_TILES // 2)
            nc.tensor.matmul_mx(
                out=bank[:, 1, :],
                lhsT=w3_w[b, w_half][:, P * w_tile : P * (w_tile + 1)].bitcast(FP8X4),
                lhsT_scale=w3_s[b, w_half][:, P * w_tile : P * (w_tile + 1)],
                rhs=x_w[b, half].bitcast(FP8X4),
                rhs_scale=x_s[b][:, cols],
                start=(b == 0),
                stop=False,
            )
            nc.tensor.matmul_mx(
                out=bank[:, 0, :],
                lhsT=w2_w[:, b, 2 * P * n : 2 * P * (n + 1)].bitcast(FP4X4),
                lhsT_scale=w2_s[:, b, P * n : P * (n + 1)],
                rhs=x_w[b, half].bitcast(FP8X4),
                rhs_scale=x_s[b][:, cols],
                start=False,
                stop=(b == H_PASSES - 1),
            )

        def finish(n, half):
            bank = score_bank[n, half]
            if (n, half) == (0, 0):
                gated = held("gated_first", [P, M_HALF], F32)
            else:
                gated = silu_pool.tile([P, M_HALF], F32, name="gated")
            nc.scalar.activation(out=gated[:], in_=bank[:, 0, :], func=ACT.Silu)
            nc.vector.tensor_tensor(out=result[half][:, n, :], in0=bank[:, 1, :], in1=gated[:], op=ALU.add)
            nc.sync.dma_start(
                out=out[P * n : P * (n + 1), half * M_HALF : (half + 1) * M_HALF], in_=result[half][:, n, :]
            )

        def w1_low(c0, width, a0, a1):
            round_w1_low(c0, width, a0, a1)
            quantise_w1_low(c0, width, a0, a1)


        load_w1_low(0, 2 * P, 0, 2)
        load_w1_low(0, 2 * P, 2, 3)
        nc.sync.dma_start(idx[:], offs)
        nc.sync.dma_start(out=d_rows[0:PACK, :], in_=d[0:PASS].rearrange("(c p) -> c p", p=P))
        for a in range(K_PASSES):
            load_tab(a)
        nc.sync.dma_start(idx4[:], offs4)
        load_page(0)
        load_gm_low(0)
        nc.sync.dma_start(idx2[:], offs2)
        nc.sync.dma_start(out=wgs_low[:], in_=wgs)
        load_page(1)
        load_gm_low(1)
        nc.sync.dma_start(idx3[:], offs3)
        load_w1_low(2 * P, 2 * P, 0, 2)
        load_w1_low(2 * P, 2 * P, 2, 3)
        load_page(2)
        load_gm_low(2)
        nc.sync.dma_start(out=d_sb[1][:], in_=d[PASS:H].rearrange("(p t) -> p t", t=PACK))

        w1_low(0, 2 * P, 0, 2)
        w1_low(0, 2 * P, 2, 3)
        d_bank = psum.tile([P, P], F32, name="bank")
        nc.tensor.transpose(d_bank[:], d_rows[:], ident[:])
        nc.vector.tensor_copy(out=d_sb[0][:], in_=d_bank[:, 0:PACK])
        gather_words(0)
        gather_scales()
        for a in range(1, K_PASSES):
            gather_words(a)
        fetch_old(0)
        h_first = held("gm_low0", [P, 2, S], F32)
        for s in range(2):
            h[s] = h_first[:, s, :]
            feature(s)
        put(0)
        fetch_old(1)
        put(1)
        w1_low(2 * P, 2 * P, 0, 2)
        w1_low(2 * P, 2 * P, 2, 3)
        load_page(3)
        load_gm_low(3)
        load_w1_high(0)
        load_w1_high(1)
        load_w1_high(2)
        load_page(4)
        load_gm_low(4)
        load_gm_low(5)
        load_page(5)
        fetch_old(2)
        x_first = held("gm_low2", [P, 2, M], F32)
        for s in range(2):
            x_low[s] = x_first[:, s, :]
            fetch_new_low(s)
        fetch_old(3)
        turn_wgs()
        feature(2)
        feature(3)
        put(2)
        for a in range(K_PASSES):
            round_w1_high(a)
            quantise_w1_high(a)
        for t in range(PACK):
            deal_wgs(t)
        x_rows[0] = held("tab_w2", [P, M // P, PASS], BF16)
        turn_x_low(0)
        turn_x_low(1)
        put(3)
        fetch_old(4)
        x_second = held("gm_low4", [P, 2, M], F32)
        for s in range(2, PACK):
            x_low[s] = x_second[:, s - 2, :]
            fetch_new_low(s)
        fetch_old(5)
        for s in range(PACK, SLICES):
            feature(s)
        feature_by_turns(6, "gm_low3")
        turn_x_low(2)
        turn_x_low(3)
        feature_by_turns(7, "h_last")
        turn_x_back(0)
        turn_x_back(1)
        put(4)
        load_page(6)
        load_gm_last()
        fetch_old(6)
        put(5)
        load_w2()
        load_w3(0)
        load_w3(1)
        load_page(7)
        for b, half in ((0, 0), (0, 1), (1, 0), (1, 1)):
            round_w3(b, half)
            if (b, half) != (0, 1):
                quantise_w3(b, half)
        put(6)
        x_w[0, 0] = held("h_mid", [P, M_HALF], U32)[:]
        quantise_x(0, 0, M_HALF)
        for n in range(N_TILES // 2):
            score_pass(n, 0, 0)
        fetch_old(7)
        x32[1, 0] = held("gm_last", [P, PACK, M_HALF], F32)[:]
        for s in range(PACK, SLICES - 1):
            fetch_new(s, 0, M_HALF)
        put(7)

        late_words = held("h_last", [P, N_HALF + M_HALF], U32)
        w3_w[0, 1] = late_words[:, 0:N_HALF]
        x_w[0, 1] = late_words[:, N_HALF : N_HALF + M_HALF]
        for half in range(2):
            x_w[1, half] = held("x_w1%d" % half, [P, M_HALF], U32)[:]
        late = held("wgs_high1", [P, PACK * M_HALF], F32)
        x32[1, M_HALF] = late[:, 0 : PACK * M_HALF].rearrange("p (t m) -> p t m", t=PACK)
        x16[1, 0] = late[:, 2 * M_HALF : PACK * M_HALF].bitcast(BF16)
        quantise_w3(0, 1)
        fetch_new(7, 0, M_HALF)
        quantise_x(0, M_HALF, M)
        round_x(1, 0, M_HALF, False)
        for n in range(N_TILES // 2, N_TILES):
            score_pass(n, 0, 0)
        for n in range(2):
            score_pass(n, 1, 0)
        for s in range(PACK, SLICES - 2):
            fetch_new(s, M_HALF, M)
        quantise_x(1, 0, M_HALF)
        for s in range(SLICES - 2, SLICES):
            fetch_new(s, M_HALF, M)
        for n in range(N_TILES):
            score_pass(n, 0, 1)
        result[0] = held("tab_w1", [P, N_TILES, M_HALF], F32)
        result[1] = held("tab_w2", [P, N_TILES, M_HALF], F32)
        finish(0, 0)
        x16[1, M_HALF] = held("gated_first", [P, M_HALF * PACK], BF16)[:]
        round_x(1, M_HALF, M, True)
        quantise_x(1, M_HALF, M)
        for n in range(1, N_TILES):
            finish(n, 0)
        for n in range(N_TILES):
            if n >= 2:
                score_pass(n, 1, 0)
            score_pass(n, 1, 1)
        for n in range(N_TILES):
            finish(n, 1)
